import numpy as np, ml_dtypes
CORES = [113,118,241,246]
N = 4
BF = ml_dtypes.bfloat16
def gentries(a):
    return np.ascontiguousarray(a.reshape(8, 16, -1).transpose(0, 2, 1)).reshape(8, -1)
def gtable(e):
    e = np.asarray(e); return np.ascontiguousarray(e.reshape(8, -1, 16).transpose(0, 2, 1)).reshape(128, -1).astype(np.int32)
V, CAP, D, R = 48, 16, 4, 2
def cube():
    P = np.indices((4, 4, 4, 4)).reshape(4, -1).T; P = P[(np.sort(P, 1) == np.arange(4)).all(1)]
    w = np.array([64, 16, 4, 1]); at = np.zeros(256, np.int64); at[P @ w] = np.arange(24)
    return at[P[:, P] @ w]
def cyclic():
    i = np.arange(24); return (i[:, None] + i) % 24
def dihedral():
    i = np.arange(24); r = i % 12; s = i // 12
    return (r[:, None] + np.where(s[:, None] == 1, -r, r)) % 12 + 12 * (s[:, None] ^ s)
def labelled(rng, plain=0, mixed=False):
    res = np.zeros((8, 24, 24), np.int64)
    for g in range(8):
        c = cyclic() if mixed and g in (2, 3) else dihedral() if mixed and g in (4, 5) else cube()
        lab = np.arange(24) if g < plain else rng.permutation(24)
        res[g][lab[:, None], lab[None, :]] = lab[c]
    return res
def values(rng):
    return rng.standard_normal((N, 128, V * 24), dtype=np.float32) * np.exp2(rng.integers(-2, 3, (N, 128, 1))).astype(np.float32)
def raw(rng, plain=0, mixed=False):
    q = (np.arange(N)[:, None, None, None] + 1 + rng.integers(0, N - 1, (N, 8, D, V))) % N
    slot = V + q * CAP + rng.integers(0, CAP, (N, 8, D, V)); own = rng.integers(0, V, (N, 8, D, V))
    return {"x": values(rng), "pose": rng.integers(0, 24, (N, 8, V)), "act": rng.integers(0, 24, (N, 8, R - 1, V)), "c": labelled(rng, plain, mixed),
            "shown": np.argsort(rng.random((N, 8, N, V)), -1)[..., :CAP], "nbr": np.where(rng.random((N, 8, D, V)) < 0.5, own, slot)}
def glists(a):
    return np.stack([gtable(v.reshape(8, -1)) for v in a])
def pack(d):
    c = d["c"]; rel = np.argsort(c, 2).transpose(0, 2, 1)
    every = lambda t: np.repeat(np.ascontiguousarray(t).reshape(1, 8, 576).astype(np.int32), N, 0)
    return {"x": np.ascontiguousarray(d["x"].astype(np.float32)), "pose": glists(d["pose"]), "act": glists(d["act"]), "rel": every(rel), "ct": every(c), "shown": glists(d["shown"]), "nbr": glists(d["nbr"])}
def setup_inputs(rng):
    return pack(raw(rng))
def setup_inputs_full(rng):
    d = raw(rng, mixed=True)
    for r in range(N):
        s = np.concatenate([V + q * CAP + np.arange(CAP) for q in range(N) if q != r])
        for g in range(8):
            flat = d["nbr"][r, g].reshape(-1).copy(); flat[rng.permutation(D * V)[:len(s)]] = s; d["nbr"][r, g] = flat.reshape(D, V)
    return pack(d)
def setup_inputs_repeat(rng):
    d = raw(rng); a, b, e, w = rng.permutation(N)[:4]; n = d["nbr"]
    n[a] = rng.integers(0, V, (8, D, V)); n[a, :, 0] = np.arange(V)
    n[b] = V + a * CAP + rng.integers(0, CAP, (8, D, V))
    n[e] = n[e][:, :1]; q0 = 1 if e == 0 else 0; q1 = N - 2 if e == N - 1 else N - 1
    n[e, :, :, 0] = 0; n[e, :, :, V - 1] = V - 1; n[e, :, :, 1] = V + q1 * CAP + CAP - 1; n[e, :, :, 2] = V + q0 * CAP
    d["shown"][w] = d["shown"][w][..., :1]
    return pack(d)
def setup_inputs_below(rng):
    d = raw(rng); k = rng.integers(0, 87, 8); k[rng.integers(0, 8)] = 86
    d["x"] = -rng.integers(1, 200, (N, 128, V * 24)).astype(np.float32) * np.repeat(np.exp2(k), 16)[:, None].astype(np.float32); return pack(d)
def setup_inputs_alike(rng):
    d = raw(rng, 2, True)
    for g in range(8):
        if g % 2 == 0:
            d["pose"][:, g] = rng.integers(0, 24); d["act"][:, g] = rng.integers(0, 24, (1, R - 1, 1))
        else:
            d["act"][:, g] = np.argmax((d["c"][g] == np.arange(24)).all(1))
    return pack(d)
def setup_inputs_spread(rng):
    d = raw(rng); k = (N, 1, V * 24)
    d["x"] = d["x"] * (np.exp2(rng.integers(-6, 7, k)) * (rng.random(k) > 0.0625)).astype(np.float32); return pack(d)
def check_inputs(d):
    bad = []; j = np.arange(24)
    def within(a, top): return bool((a >= 0).all() and (a < top).all())
    if not np.isfinite(d["x"]).all(): bad.append("finite")
    elif not (np.abs(d["x"]) <= 2.0 ** 94).all(): bad.append("size")
    if not within(d["pose"], 24): bad.append("pose")
    if not within(d["act"], 24): bad.append("act")
    if not within(d["shown"], V): bad.append("shown")
    for r in range(N):
        n = d["nbr"][r]
        if not within(n, V + N * CAP) or ((n >= V + r * CAP) & (n < V + r * CAP + CAP)).any(): bad.append("nbr"); break
    if not (d["rel"] == d["rel"][:1]).all() or not (d["ct"] == d["ct"][:1]).all(): bad.append("tables_alike")
    if not within(d["rel"], 24) or not within(d["ct"], 24): bad.append("tables_range")
    else:
        for g in range(8):
            c = d["ct"][0, g].reshape(24, 24).astype(np.int64); l = d["rel"][0, g].reshape(24, 24).astype(np.int64)
            if not ((np.sort(c, 1) == j).all() and (np.sort(c, 0) == j[:, None]).all() and (c[c] == c[:, c]).all()): bad.append("ct_group"); break
            if not (c[j[None, :], l] == j[:, None]).all(): bad.append("rel"); break
    return bad
def reference(x, pose, act, rel, ct, shown, nbr):
    f = x.reshape(N, 8, 16, V, 24)
    p = np.stack([gentries(v) for v in pose]).astype(np.int64)
    ac = np.stack([gentries(v) for v in act]).reshape(N, 8, R - 1, V).astype(np.int64)
    sh = np.stack([gentries(v) for v in shown]).reshape(N, 8, N, CAP)
    nb = np.stack([gentries(v) for v in nbr]).reshape(N, 8, D, V)
    for t in range(R):
        new = np.zeros(f.shape, np.float32); turned = np.zeros(p.shape, np.int64)
        for r in range(N):
            for g in range(8):
                fe = np.concatenate([f[r, g]] + [f[q, g][:, sh[q, g, r]] for q in range(N)], 1)
                pe = np.concatenate([p[r, g]] + [p[q, g][sh[q, g, r]] for q in range(N)])
                j = nb[r, g]
                e = rel[r, g][p[r, g][None, :] * 24 + pe[j]].astype(np.int64)
                k = ct[r, g][e[:, :, None] * 24 + np.arange(24)]
                new[r, g] = np.maximum.reduce(fe[:, j[:, :, None], k], axis=1)
                if t < R - 1: turned[r, g] = ct[r, g][p[r, g] * 24 + ac[r, g, t]]
        f = new; p = turned
    return {"y": np.ascontiguousarray(f.reshape(N, 128, V * 24))}

@@ -1,0 +1,362 @@
+from concourse.bass import DstId, RemoteDMATransfer
+from concourse.mybir import AluOpType, AxisListType, ActivationFunctionType
+
+NX = 140
+SCRATCH = {
+    "X": ("sbuf", [128, 1152], "float32"), "TR": ("sbuf", [128, 48], "int32"), "PO": ("sbuf", [128, 4], "int32"),
+    "SHN": ("sbuf", [128, 4], "int32"), "NB": ("sbuf", [128, 12], "int32"), "AC": ("sbuf", [128, 4], "int32"),
+    "CT": ("sbuf", [128, 48], "int32"),
+    "IP": ("sbuf", [128, 2], "int32"), "DD": ("sbuf", [128, 128], "float32"), "GI": ("sbuf", [128, 128], "float32"),
+    "IM": ("sbuf", [128, 16], "int32"), "IM2": ("sbuf", [128, 16], "int32"), "MK": ("sbuf", [128, 16], "float32"),
+    "C48": ("sbuf", [128, 96], "float32"), "S4": ("sbuf", [128, 4], "float32"),
+    "SQ4": ("sbuf", [128, 4], "float32"), "N4": ("sbuf", [128, 4], "float32"), "NP": ("sbuf", [128, 4], "float32"),
+    "NM": ("sbuf", [128, 4], "float32"), "AT": ("sbuf", [128, 112], "float32"), "I24": ("sbuf", [128, 24], "float32"),
+    "B1": ("sbuf", [128, 2], "int32"), "B8": ("sbuf", [128, 2], "int32"), "BQ": ("sbuf", [128, 2], "int32"),
+    "BG": ("sbuf", [128, 2], "int32"), "PG": ("sbuf", [128, 1], "float32"), "QF": ("sbuf", [128, 2], "float32"),
+    "LO": ("sbuf", [128, 1], "float32"), "HI": ("sbuf", [128, 1], "float32"), "PQ": ("sbuf", [128, 2], "float32"),
+    "PQ4": ("sbuf", [128, 2], "float32"),
+    "SH": ("sbuf", [128, 128], "float16"), "SL": ("sbuf", [128, 128], "float16"), "ON": ("sbuf", [128, 128], "bfloat16"),
+    "SHW": ("sbuf", [128, 128], "float32"), "SLW": ("sbuf", [128, 128], "float32"), "ID": ("sbuf", [128, 128], "float32"),
+    "RN": ("sbuf", [128, 256], "bfloat16"), "BL": ("sbuf", [128, 32], "uint16"),
+    "WT": ("sbuf", [128, 48], "float32"), "LP": ("sbuf", [128, 6], "uint16"),
+    "NN": ("sbuf", [128, 96], "float32"), "LSH": ("sbuf", [128, 6], "uint16"), "SHF": ("sbuf", [128, 4], "float32"),
+    "RR": ("sbuf", [128, 96], "float16"),
+    "LA": ("sbuf", [128, 72], "uint16"), "OWN": ("sbuf", [128, 72], "uint16"),
+    "NBU": ("sbuf", [128, 12], "uint16"), "IT": ("sbuf", [128, 16], "float32"), "IDC": ("sbuf", [128, 1], "float32"),
+    "LM": ("sbuf", [128, 6], "uint16"), "CW": ("sbuf", [128, 64], "float32"), "BD": ("sbuf", [128, 512], "bfloat16"),
+    "TRG": ("sbuf", [128, 96], "float32"), "MS": ("sbuf", [128, 96], "float32"),
+    "OA": ("sbuf", [128, 96], "bfloat16"), "OV": ("sbuf", [128, 96], "bfloat16"), "OK": ("sbuf", [128, 96], "bfloat16"),
+    "ARM": ("sbuf", [128, 192], "float32"), "Z": ("sbuf", [128, 384], "float32"), "ZY": ("sbuf", [128, 384], "float32"),
+    "LS1": ("sbuf", [128, 12], "uint16"), "LS2": ("sbuf", [128, 12], "uint16"),
+    "ZS1": ("sbuf", [128, 192], "float32"), "ZS2": ("sbuf", [128, 192], "float16"),
+    "LB": ("sbuf", [128, 288], "uint16"), "LC": ("sbuf", [128, 288], "uint16"), "LY": ("sbuf", [128, 288], "uint16"),
+    "W0": ("sbuf", [128, 2304], "float32"), "W1": ("sbuf", [128, 2304], "float32"),
+    "SA": ("sbuf", [128, 1152], "float32"), "YB": ("sbuf", [128, 1152], "float32"),
+    "F0": ("sbuf", [128, 1152], "float32"), "F1": ("sbuf", [128, 1152], "float32"),
+    "F2": ("sbuf", [128, 1152], "float32"), "F3": ("sbuf", [128, 1152], "float32"),
+    "G2": ("sbuf", [128, 2304], "float32"), "G3": ("sbuf", [128, 2304], "float32"),
+    "H0": ("sbuf", [128, 2304], "float32"), "H1": ("sbuf", [128, 2304], "float32"), "H2": ("sbuf", [128, 2304], "float32"),
+    "PT": ("psum", [128, 512], "float32"), "PY": ("psum", [128, 512], "float32"), "PV": ("psum", [128, 512], "float32"),
+    "PK": ("psum", [128, 512], "float32"), "PM": ("psum", [128, 512], "float32"),
+    "PC0": ("psum", [128, 512], "float32"), "PC1": ("psum", [128, 512], "float32"), "PC2": ("psum", [128, 512], "float32"),
+}
+SEMAPHORES = ["left"] + ["arr%d_%d" % (t, q) for t in range(2) for q in range(4)] + ["x%d" % k for k in range(NX)]
+OWNW, SLW = 48 * 24, 16 * 24
+JOBS0 = [8, 12, 12, 16]
+JOBS1 = [8, 12, 16, 12]
+
+
+def place(q, p):
+    return OWNW + SLW * (q if q < p else q - 1)
+
+
+def rank_program(g, core, T, topo):
+    r = T.rank_of(core)
+    if r is None:
+        return
+    A, ACT = AluOpType, ActivationFunctionType
+    ops = []
+
+    def op(q, f, deps=(), kind="c"):
+        ops.append({"q": q, "f": f, "deps": list(deps), "kind": kind, "grp": len(ops)})
+        return len(ops) - 1
+
+    def join(*ks):
+        for k in ks:
+            ops[k]["grp"] = ks[0]
+        return list(ks)
+
+    v, s, t = g.vector, g.scalar, g.tensor
+    queues = {"v": v, "s": s, "t": t, "g": g, "y": g.sync}
+
+    def ts(out, in0, s1, op0, s2=None, op1=None, deps=()):
+        if op1 is None:
+            return op("v", lambda: v.tensor_scalar(out, in0, s1, None, op0), deps)
+        return op("v", lambda: v.tensor_scalar(out, in0, s1, s2, op0, op1), deps)
+
+    def tt(out, a, b, o, deps=()):
+        return op("v", lambda: v.tensor_tensor(out, a, b, o), deps)
+
+    def cp(out, a, deps=()):
+        return op("v", lambda: v.tensor_copy(out, a), deps)
+
+    def ac(out, a, deps=()):
+        return op("s", lambda: s.activation(out, a, ACT.Copy), deps)
+
+    def mm(out, lhs, rhs, start, stop, deps):
+        return op("t", lambda: t.matmul(out, lhs, rhs, start, stop), deps)
+
+    def ld(q, out, in_, deps=()):
+        return op(q, lambda: queues[q].dma_start(out, in_), deps, "d")
+
+    others = [p for p in range(len(T.cores)) if p != r]
+    near = [p for p in others if T.cores[p] in topo.cores_of(core)]
+    far = [p for p in others if p not in near]
+    far.sort(key=lambda p: topo.die(T.cores[p]) != topo.die(core))
+    dest = far + near
+    feng = topo.engines(core, T.cores[far[0]])
+    neng = [e for e in topo.engines(core, T.cores[near[0]]) if e not in feng]
+
+    def bits(es):
+        return sum(1 << e for e in es)
+
+    d_ra = ld("y", T.TR[:, 0:24], T.rel[:, 0:384])
+    d_po = ld("s", T.PO[:, 0:3], T.pose[:, :])
+    d_rd = ld("y", T.TR[:, 24:48], T.rel[:, 192:576])
+    d_sh = ld("s", T.SHN[:, 0:4], T.shown[:, :])
+    d_x = ld("s", T.X[:, :], T.x[:, :])
+    d_ac = ld("s", T.AC[:, 0:3], T.act[:, :])
+    d_nb = ld("s", T.NB[:, 0:12], T.nbr[:, :])
+    d_ct = join(ld("s", T.CT[:, 0:24], T.ct[:, 0:384]), ld("s", T.CT[:, 24:48], T.ct[:, 192:576]))
+    join(d_ra, d_rd)
+
+    def iota(out, pat, base, cm, f32=True):
+        if f32:
+            return op("g", lambda: g.iota(out, pat, base, cm, allow_small_or_imprecise_dtypes=True))
+        return op("g", lambda: g.iota(out, pat, base, cm))
+
+    i_p = iota(T.IP[:, :], [[0, 2]], 0, 1, False)
+    i_d = iota(T.DD[:, :], [[1, 128]], 0, -1)
+    i_c = iota(T.C48[:, :], [[0, 2], [24, 48]], 0, 0)
+    i_m = iota(T.IM[:, :], [[1, 16]], 0, -1, False)
+    i_g = iota(T.GI[:, :], [[1, 8], [0, 16]], 0, 0)
+    i_4 = iota(T.S4[:, :], [[24, 2], [8, 2]], -48, 0)
+    i_24 = iota(T.I24[:, :], [[1, 24]], 0, 0)
+    i_n = iota(T.N4[:, :], [[48, 4]], 0, 0)
+    hole = 48 + 16 * r + 16
+    i_a = [iota(T.AT[:, 0:hole], [[24, hole]], 0, 0)]
+    if hole < 112:
+        i_a.append(iota(T.AT[:, hole:112], [[24, 112 - hole]], 24 * (hole - 16), 0))
+    join(*i_a)
+
+    c_b = join(ts(T.B1[:, :], T.IP[:, :], 1, A.bitwise_and, deps=[i_p]),
+               ts(T.B8[:, :], T.IP[:, :], 8, A.bitwise_and, deps=[i_p]),
+               ts(T.BQ[:, :], T.IP[:, :], 15, A.bitwise_and, deps=[i_p]),
+               ts(T.BG[:, :], T.IP[:, :], 4, A.arith_shift_right, deps=[i_p]))
+    c_m = join(ts(T.LO[:, :], T.B8[:, 0:1], 0, A.is_equal, deps=c_b),
+               ts(T.HI[:, :], T.B8[:, 0:1], 0, A.is_gt, deps=c_b),
+               ts(T.PQ[:, 0:1], T.B1[:, 0:1], 48, A.mult, deps=c_b),
+               ts(T.PQ[:, 1:2], T.B1[:, 0:1], -48, A.mult, 48, A.add, deps=c_b),
+               cp(T.PG[:, :], T.BG[:, 0:1], deps=c_b),
+               cp(T.QF[:, 0:1], T.BQ[:, 0:1], deps=c_b))
+    c_s = join(ts(T.SH[:, :], T.DD[:, :], -8, A.is_equal, T.HI[:, :], A.mult, deps=[i_d] + c_m),
+               ts(T.SL[:, :], T.DD[:, :], 8, A.is_equal, T.LO[:, :], A.mult, deps=[i_d] + c_m))
+    c_f = join(ts(T.SHW[:, :], T.DD[:, :], -8, A.is_equal, T.HI[:, :], A.mult, deps=[i_d] + c_m),
+               ts(T.SLW[:, :], T.DD[:, :], 8, A.is_equal, T.LO[:, :], A.mult, deps=[i_d] + c_m))
+    im2 = ts(T.IM2[:, :], T.IM[:, :], 15, A.bitwise_and, deps=[i_m])
+    zc = op("v", lambda: v.memset(T.CW[:, 48:64], 0.0))
+    mk = ts(T.MK[:, :], T.IM2[:, :], 0, A.is_equal, deps=[im2])
+    c_q = ts(T.QF[:, 1:2], T.QF[:, 0:1], 8, A.add, T.HI[:, :], A.mult, deps=c_m)
+    on = ts(T.ON[:, :], T.GI[:, :], T.PG[:, :], A.is_equal, deps=[i_g] + c_m)
+    sq4 = ts(T.SQ4[:, :], T.S4[:, :], T.QF[:, 0:1], A.add, deps=[i_4] + c_m)
+
+    lp = join(*[ts(T.LP[:, 3 * k:3 * k + 3], T.PO[:, 0:3], 24 * k, A.add, deps=[d_po]) for k in range(2)])
+    nn = tt(T.NN[:, :], T.TR[:, :].indirect(T.LP[:, 0:6]), T.C48[:, :], A.add, deps=lp + [d_ra, d_rd, i_c])
+    shf = cp(T.SHF[:, :], T.SHN[:, :], deps=[d_sh])
+    wt = cp(T.WT[:, :], T.TR[:, :], deps=[d_ra, d_rd])
+    lsh = join(*[ts(T.LSH[:, k::3], T.PQ[:, :], T.SHF[:, p:p + 1], A.add, deps=c_m + [shf]) for k, p in enumerate(dest)])
+    rr = cp(T.RR[:, :], T.NN[:, :].indirect(T.LSH[:, 0:6]), deps=[nn] + lsh)
+    trg = ac(T.TRG[:, :], T.WT[:, :].indirect(T.LP[:, 0:6]), deps=lp + [wt])
+    idt = tt(T.IT[:, :], T.WT[:, 0:16], T.MK[:, :], A.mult, deps=[wt, mk])
+    la = [cp(T.LA[:, 0::3], T.RR[:, 0:48:2], deps=[rr]), cp(T.LA[:, 2::3], T.RR[:, 1:48:2], deps=[rr])]
+    qa = join(mm(T.PT[:, 0:24], T.SH[:, :], T.RR[:, 48:96:2], True, False, [rr] + c_s),
+              mm(T.PT[:, 0:24], T.SL[:, :], T.RR[:, 49:96:2], False, True, [rr] + c_s))
+    idc = op("v", lambda: v.tensor_reduce(T.IDC[:, :], T.IT[:, :], AxisListType.X, A.add), [idt])
+    qo = join(mm(T.PM[:, 0:24], T.SHW[:, :], T.NN[:, 48:96:2], True, False, [nn] + c_f),
+              mm(T.PM[:, 0:24], T.SLW[:, :], T.NN[:, 1:48:2], False, True, [nn] + c_f))
+    ow = [cp(T.OWN[:, 0::3], T.NN[:, 0:48:2], deps=[nn])]
+    la.append(cp(T.LA[:, 1::3], T.PT[:, 0:24], deps=qa))
+    join(*la)
+
+    bl = join(*[ts(T.BL[:, 8 * k:8 * k + 8], T.ON[:, 0::16], T.SQ4[:, k:k + 1], A.mult, 48, A.add, deps=[on, sq4]) for k in range(4)])
+    ow.append(cp(T.OWN[:, 2::3], T.NN[:, 49:96:2], deps=[nn]))
+    ow.append(cp(T.OWN[:, 1::3], T.PM[:, 0:24], deps=qo))
+    join(*ow)
+
+    def transfer(p, srcs, win, es, arr, alu=0):
+        rid, pid = topo.addr(T.cores[p], core)
+        c = place(r, p)
+        return RemoteDMATransfer(srcs=srcs, dsts=[win[:, c:c + SLW]], dst_ids=[DstId(rid=rid, pnc=pid)],
+                                 dma_engine_mask=bits(es), remote_sem=T.sem[arr], alu_op=alu)
+
+    left = [0]
+
+    def send(p, srcs, win, arr, alu, deps):
+        es = feng if p in far else neng
+        left[0] += len(es)
+        x = transfer(p, srcs, win, es, arr, alu)
+        return op("g", lambda: g.remote_dma_fused([x], local_sem=T.sem["left"]), deps, "r")
+
+    for k, p in enumerate(dest):
+        a, b = SLW * k, SLW * k + SLW // 2
+        x = join(cp(T.SA[:, a:b], T.X[:, :].indirect(T.LA[:, 24 * k:24 * k + 12]), deps=la + [d_x]),
+                 ac(T.SA[:, b:a + SLW], T.X[:, :].indirect(T.LA[:, 24 * k + 12:24 * k + 24]), deps=la + [d_x]))
+        send(p, [T.SA[:, a:a + SLW]], T.W0, "arr0_%d" % r, 0, x)
+    arr0, arr1 = [[("sem", "arr%d_%d" % (k, q), len(feng) if q in far else len(neng)) for q in others] for k in range(2)]
+
+    lm = join(*[cp(T.LM[:, 3 * k:3 * k + 3], T.AC[:, 0:3], deps=[d_ac]) for k in range(2)])
+    cw = join(cp(T.CW[:, 0:24], T.CT[:, 0:24], deps=d_ct), ts(T.CW[:, 24:48], T.CT[:, 24:48], T.HI[:, :], A.mult, deps=d_ct + c_m))
+    ms = ac(T.MS[:, :], T.I24[:, :].indirect(T.LM[:, :]), deps=lm + [i_24])
+    nbu = cp(T.NBU[:, :], T.NB[:, :], deps=[d_nb])
+    bd = join(ac(T.BD[:, 0:256], T.CW[:, :].indirect(T.BL[:, 0:16]), deps=bl + cw + [zc]),
+              cp(T.BD[:, 256:512], T.CW[:, :].indirect(T.BL[:, 16:32]), deps=bl + cw + [zc]))
+    oa = tt(T.OA[:, :], T.TRG[:, :], T.MS[:, :], A.is_equal, deps=[trg, ms])
+    arm = ac(T.ARM[:, :], T.AT[:, :].indirect(T.NBU[:, :]), deps=i_a + [nbu])
+
+    def rows(out, oh, deps):
+        return join(*[mm(out[:, 48 * h:48 * h + 48], T.BD[:, 256 * k + 128 * h:256 * k + 128 * h + 128], oh[:, 48 * k:48 * k + 48],
+                         k == 0, k == 1, deps) for h in range(2) for k in range(2)])
+
+    def plus(out, P, deps):
+        return join(*[tt(out[:, 192 * h + 48 * n:192 * h + 48 * n + 48], T.ARM[:, 48 * n:48 * n + 48], P[:, 48 * h:48 * h + 48], A.add, deps)
+                      for h in range(2) for n in range(4)])
+
+    def middle(P, up, down, even, odd, deps):
+        return join(mm(P, up, even, True, False, deps), mm(P, down, odd, False, True, deps))
+
+    qy = rows(T.PY, T.OA, [oa] + bd)
+    c_r = join(ts(T.RN[:, 0:128], T.ON[:, :], T.QF[:, 0:1], A.mult, deps=[on] + c_m),
+               ts(T.RN[:, 128:256], T.ON[:, :], T.QF[:, 1:2], A.mult, deps=[on, c_q]))
+    c_p = ts(T.PQ4[:, :], T.PQ[:, :], 4, A.mult, deps=c_m)
+    idm = ts(T.ID[:, :], T.DD[:, :], 0, A.is_equal, deps=[i_d])
+    c_np = join(ts(T.NP[:, :], T.N4[:, :], T.PQ4[:, 0:1], A.add, deps=[i_n, c_p]),
+                ts(T.NM[:, :], T.N4[:, :], T.PQ4[:, 1:2], A.add, deps=[i_n, c_p]))
+    own0 = [ac(T.W0[:, 0:OWNW], T.X[:, :].indirect(T.OWN[:, :]), deps=ow + [d_x])]
+    ov = ts(T.OV[:, :], T.PY[:, 0:96], T.IDC[:, :], A.is_equal, deps=qy + [idc])
+    qv = join(*[mm(T.PV[:, 48 * h:48 * h + 48], T.RN[:, 128 * k:128 * k + 128], T.OV[:, 48 * k:48 * k + 48], k == 0, k == 1, [ov] + c_r)
+                for h in range(2) for k in range(2)])
+    zy = plus(T.ZY, T.PY, qy + [arm])
+    ok = tt(T.OK[:, :], T.TRG[:, :], T.PV[:, 0:96], A.is_equal, deps=qv + [trg])
+    qk = rows(T.PK, T.OK, [ok] + bd)
+    ls = join(*([ts(T.LS2[:, 4 * k:4 * k + 4], T.NM[:, :], T.SHF[:, p:p + 1], A.add, deps=c_np + [shf]) for k, p in enumerate(dest)] +
+                [ts(T.LS1[:, 4 * k:4 * k + 4], T.NP[:, :], T.SHF[:, p:p + 1], A.add, deps=c_np + [shf]) for k, p in enumerate(dest)]))
+    qz = middle(T.PV[:, 0:96], T.SHW[:, :], T.SLW[:, :], T.ZY[:, 192:384:2], T.ZY[:, 1:192:2], zy + c_f + [ok])
+    ly = [cp(T.LY[:, 0::3], T.ZY[:, 0:192:2], deps=zy)]
+    z = plus(T.Z, T.PK, qk + [arm])
+    ly.append(cp(T.LY[:, 2::3], T.ZY[:, 193:384:2], deps=zy))
+    zs2 = ts(T.ZS2[:, :], T.Z[:, :].indirect(T.LS2[:, :]), -OWNW, A.add, deps=z + ls)
+    zs1 = ac(T.ZS1[:, :], T.Z[:, :].indirect(T.LS1[:, :]), deps=z + ls)
+    qb = middle(T.PM[:, 0:96], T.SH[:, :], T.SL[:, :], T.ZS2[:, 0::2], T.ZS2[:, 1::2], [zs2] + c_s + ow)
+    qc = middle(T.PT[:, 0:96], T.SHW[:, :], T.SLW[:, :], T.Z[:, 192:384:2], T.Z[:, 1:192:2], z + c_f + la)
+    ly.append(cp(T.LY[:, 1::3], T.PV[:, 0:96], deps=qz))
+    join(*ly)
+    lc = [cp(T.LC[:, 0::3], T.Z[:, 0:192:2], deps=z), cp(T.LC[:, 2::3], T.Z[:, 193:384:2], deps=z)]
+    lb = join(ts(T.LB[:, 1::3], T.PM[:, 0:96], OWNW, A.add, deps=qb),
+              cp(T.LB[:, 0::3], T.ZS1[:, 0::2], deps=[zs1]), cp(T.LB[:, 2::3], T.ZS1[:, 1::2], deps=[zs1]))
+
+    for k, p in enumerate(dest):
+        lists = [T.LB[:, 96 * k + 24 * n:96 * k + 24 * n + 24] for n in range(4)]
+        f0, f1, f2, f3 = [T[x][:, SLW * k:SLW * k + SLW] for x in ("F0", "F1", "F2", "F3")]
+        deps = lb + own0 + arr0
+        if k == 2:
+            lc.append(cp(T.LC[:, 1::3], T.PT[:, 0:96], deps=qc))
+            join(*lc)
+        hw = SLW // 2
+        x0 = [cp(f0[:, hw * h:hw * h + hw], T.W0[:, :].indirect(lists[0][:, 12 * h:12 * h + 12]), deps) for h in range(2)]
+        x1 = [tt(f1[:, hw * h:hw * h + hw], T.W0[:, :].indirect(lists[1][:, 12 * h:12 * h + 12]), f0[:, hw * h:hw * h + hw], A.max,
+                 deps + [x0[h]]) for h in range(2)]
+        x = join(*x1, ac(f2, T.W0[:, :].indirect(lists[2]), deps), ac(f3, T.W0[:, :].indirect(lists[3]), deps))
+        send(p, [f1, f2, f3], T.W1, "arr1_%d" % r, 2, x)
+
+    banks = [[T.PC0, []], [T.PC1, []], [T.PC2, []], [T.PM, lb], [T.PT, lc], [T.PK, z], [T.PV, ly], [T.PY, zy]]
+    spare, turn = [0], [0]
+
+    def pieces(win, lists, jobs, deps, out, stored):
+        js, at = [], 0
+        for nodes in jobs:
+            w, c = nodes * 24, spare[0]
+            src = [win[:, :].indirect(lists[:, 72 * n + at // 2 * 3:72 * n + (at + nodes) // 2 * 3]) for n in range(4)]
+            js.append({"w": w, "src": src, "out": out[:, at * 24:(at + nodes) * 24]})
+            js[-1].update({x: T[x][:, c:c + w] for x in ("G2", "G3", "H0", "H1", "H2")})
+            spare[0] += w
+            at += nodes
+
+        def third(j):
+            g3 = ac(j["G3"], j["src"][3], deps)
+            bank = banks[turn[0] % len(banks)]
+            turn[0] += 1
+            j["P"] = bank[0][:, 0:j["w"]]
+            if j is js[-1]:
+                j["p"] = ac(j["P"], j["G3"], [g3] + bank[1])
+            else:
+                j["p"] = mm(j["P"], T.ID[:, :], j["G3"], True, True, [g3, idm] + bank[1])
+            j["bank"] = bank
+        for k, j in enumerate(js[1:]):
+            j["g"] = ac(j["G2"], j["src"][2], deps)
+            if k == 0:
+                third(js[0])
+            third(j)
+
+        res = []
+
+        def first(j):
+            j["h"] = tt(j["H1"], j["src"][0], j["G2"], A.max, deps + [j["g"]])
+
+        def second(j):
+            j["h"] = tt(j["H2"], j["src"][2 if j is js[0] else 1], j["H1"], A.max, deps + [j["h"]])
+
+        def last(k):
+            j = js[k]
+            e = tt(j["out"], j["H2"], j["P"], A.max, [j["h"], j["p"]])
+            j["bank"][1] = [e]
+            res.append(e)
+            if stored:
+                stored(k, e)
+        h = cp(js[0]["H0"], js[0]["src"][0], deps)
+        js[0]["h"] = tt(js[0]["H1"], js[0]["src"][1], js[0]["H0"], A.max, deps + [h])
+        first(js[1])
+        second(js[0])
+        n = len(js)
+        if stored:
+            second(js[1])
+            last(0)
+            for k in range(2, n):
+                first(js[k])
+                last(k - 1)
+                second(js[k])
+        else:
+            for k in range(2, n):
+                first(js[k])
+                second(js[k - 1])
+                last(k - 2)
+            second(js[n - 1])
+            last(n - 2)
+        last(n - 1)
+        return res
+
+    own1 = pieces(T.W0, T.LC, JOBS0, lc + own0 + arr0, T.W1, None)
+
+    stores = []
+
+    def store(k, m):
+        a, b = sum(JOBS1[:k]) * 24, sum(JOBS1[:k + 1]) * 24
+        stores.append(ld("y", T.y[:, a:b], T.YB[:, a:b], [m]))
+
+    pieces(T.W1, T.LY, JOBS1, ly + own1 + arr1, T.YB, store)
+    op("y", None, stores, "w")
+    op("g", None, [("sem", "left", left[0])], "w")
+
+    used, total = set(), {}
+    for o in ops:
+        used.update(ops[d]["grp"] for d in o["deps"] if not isinstance(d, tuple))
+    for o in ops:
+        total[o["grp"]] = total.get(o["grp"], 0) + (16 if o["kind"] == "d" else 1)
+    names = {k: "x%d" % n for n, k in enumerate(sorted(used))}
+    done = {q: {} for q in queues}
+
+    def wait(q, name, val):
+        if done[q].get(name, 0) < val:
+            queues[q].wait_ge(T.sem[name], val)
+            done[q][name] = val
+
+    for o in ops:
+        for d in o["deps"]:
+            if isinstance(d, tuple):
+                wait(o["q"], d[1], d[2])
+            else:
+                k = ops[d]["grp"]
+                wait(o["q"], names[k], total[k])
+        if o["kind"] != "w":
+            ins = o["f"]()
+            if o["grp"] in names:
+                ins.then_inc(T.sem[names[o["grp"]]], 16 if o["kind"] == "d" else 1)

@@ -1,53 +1,54 @@
 from concourse.bass import DstId, RemoteDMATransfer
-from concourse.mybir import AluOpType, AxisListType, ActivationFunctionType
+from concourse.mybir import AluOpType, ActivationFunctionType
 
-NX = 140
+NX = 144
 SCRATCH = {
     "X": ("sbuf", [128, 1152], "float32"), "TR": ("sbuf", [128, 48], "int32"), "PO": ("sbuf", [128, 4], "int32"),
-    "SHN": ("sbuf", [128, 4], "int32"), "NB": ("sbuf", [128, 12], "int32"), "AC": ("sbuf", [128, 4], "int32"),
-    "CT": ("sbuf", [128, 48], "int32"),
+    "NB": ("sbuf", [128, 16], "int32"), "AC": ("sbuf", [128, 4], "int32"), "CT": ("sbuf", [128, 48], "int32"),
     "IP": ("sbuf", [128, 2], "int32"), "DD": ("sbuf", [128, 128], "float32"), "GI": ("sbuf", [128, 128], "float32"),
-    "IM": ("sbuf", [128, 16], "int32"), "IM2": ("sbuf", [128, 16], "int32"), "MK": ("sbuf", [128, 16], "float32"),
-    "C48": ("sbuf", [128, 96], "float32"), "S4": ("sbuf", [128, 4], "float32"),
-    "SQ4": ("sbuf", [128, 4], "float32"), "N4": ("sbuf", [128, 4], "float32"), "NP": ("sbuf", [128, 4], "float32"),
-    "NM": ("sbuf", [128, 4], "float32"), "AT": ("sbuf", [128, 112], "float32"), "I24": ("sbuf", [128, 24], "float32"),
+    "C48": ("sbuf", [128, 96], "float32"), "CB": ("sbuf", [128, 48], "bfloat16"), "S4": ("sbuf", [128, 4], "float32"),
+    "SQ4": ("sbuf", [128, 4], "float32"), "AT": ("sbuf", [128, 112], "float32"), "I48": ("sbuf", [128, 48], "float32"),
     "B1": ("sbuf", [128, 2], "int32"), "B8": ("sbuf", [128, 2], "int32"), "BQ": ("sbuf", [128, 2], "int32"),
+    "B7": ("sbuf", [128, 2], "int32"), "QR": ("sbuf", [128, 1], "float32"),
     "BG": ("sbuf", [128, 2], "int32"), "PG": ("sbuf", [128, 1], "float32"), "QF": ("sbuf", [128, 2], "float32"),
     "LO": ("sbuf", [128, 1], "float32"), "HI": ("sbuf", [128, 1], "float32"), "PQ": ("sbuf", [128, 2], "float32"),
-    "PQ4": ("sbuf", [128, 2], "float32"),
     "SH": ("sbuf", [128, 128], "float16"), "SL": ("sbuf", [128, 128], "float16"), "ON": ("sbuf", [128, 128], "bfloat16"),
     "SHW": ("sbuf", [128, 128], "float32"), "SLW": ("sbuf", [128, 128], "float32"), "ID": ("sbuf", [128, 128], "float32"),
+    "SHB": ("sbuf", [128, 128], "bfloat16"), "SLB": ("sbuf", [128, 128], "bfloat16"), "IDB": ("sbuf", [128, 128], "bfloat16"),
+    "LOB": ("sbuf", [128, 128], "bfloat16"), "HIB": ("sbuf", [128, 128], "bfloat16"),
+    "L24": ("sbuf", [128, 128], "bfloat16"), "H24": ("sbuf", [128, 128], "bfloat16"),
     "RN": ("sbuf", [128, 256], "bfloat16"), "BL": ("sbuf", [128, 32], "uint16"),
-    "WT": ("sbuf", [128, 48], "float32"), "LP": ("sbuf", [128, 6], "uint16"),
-    "NN": ("sbuf", [128, 96], "float32"), "LSH": ("sbuf", [128, 6], "uint16"), "SHF": ("sbuf", [128, 4], "float32"),
-    "RR": ("sbuf", [128, 96], "float16"),
-    "LA": ("sbuf", [128, 72], "uint16"), "OWN": ("sbuf", [128, 72], "uint16"),
-    "NBU": ("sbuf", [128, 12], "uint16"), "IT": ("sbuf", [128, 16], "float32"), "IDC": ("sbuf", [128, 1], "float32"),
-    "LM": ("sbuf", [128, 6], "uint16"), "CW": ("sbuf", [128, 64], "float32"), "BD": ("sbuf", [128, 512], "bfloat16"),
-    "TRG": ("sbuf", [128, 96], "float32"), "MS": ("sbuf", [128, 96], "float32"),
-    "OA": ("sbuf", [128, 96], "bfloat16"), "OV": ("sbuf", [128, 96], "bfloat16"), "OK": ("sbuf", [128, 96], "bfloat16"),
-    "ARM": ("sbuf", [128, 192], "float32"), "Z": ("sbuf", [128, 384], "float32"), "ZY": ("sbuf", [128, 384], "float32"),
-    "LS1": ("sbuf", [128, 12], "uint16"), "LS2": ("sbuf", [128, 12], "uint16"),
-    "ZS1": ("sbuf", [128, 192], "float32"), "ZS2": ("sbuf", [128, 192], "float16"),
-    "LB": ("sbuf", [128, 288], "uint16"), "LC": ("sbuf", [128, 288], "uint16"), "LY": ("sbuf", [128, 288], "uint16"),
-    "W0": ("sbuf", [128, 2304], "float32"), "W1": ("sbuf", [128, 2304], "float32"),
-    "SA": ("sbuf", [128, 1152], "float32"), "YB": ("sbuf", [128, 1152], "float32"),
-    "F0": ("sbuf", [128, 1152], "float32"), "F1": ("sbuf", [128, 1152], "float32"),
-    "F2": ("sbuf", [128, 1152], "float32"), "F3": ("sbuf", [128, 1152], "float32"),
-    "G2": ("sbuf", [128, 2304], "float32"), "G3": ("sbuf", [128, 2304], "float32"),
-    "H0": ("sbuf", [128, 2304], "float32"), "H1": ("sbuf", [128, 2304], "float32"), "H2": ("sbuf", [128, 2304], "float32"),
-    "PT": ("psum", [128, 512], "float32"), "PY": ("psum", [128, 512], "float32"), "PV": ("psum", [128, 512], "float32"),
-    "PK": ("psum", [128, 512], "float32"), "PM": ("psum", [128, 512], "float32"),
-    "PC0": ("psum", [128, 512], "float32"), "PC1": ("psum", [128, 512], "float32"), "PC2": ("psum", [128, 512], "float32"),
+    "LP": ("sbuf", [128, 6], "uint16"), "LM": ("sbuf", [128, 6], "uint16"),
+    "NN": ("sbuf", [128, 96], "float32"), "LSH": ("sbuf", [128, 8], "uint16"),
+    "RR": ("sbuf", [128, 128], "float16"), "LA": ("sbuf", [128, 96], "uint16"), "OWN": ("sbuf", [128, 72], "uint16"),
+    "NBU": ("sbuf", [128, 16], "uint16"), "CW": ("sbuf", [128, 64], "float32"), "BD": ("sbuf", [128, 512], "bfloat16"),
+    "AS": ("sbuf", [128, 96], "float32"), "MS": ("sbuf", [128, 96], "float32"), "CA": ("sbuf", [128, 96], "float32"),
+    "OA": ("sbuf", [128, 96], "bfloat16"), "OS": ("sbuf", [128, 96], "bfloat16"), "OK": ("sbuf", [128, 96], "bfloat16"),
+    "ARM": ("sbuf", [128, 256], "bfloat16"), "RW": ("sbuf", [128, 96], "bfloat16"), "UU": ("sbuf", [128, 288], "bfloat16"),
+    "LC": ("sbuf", [128, 288], "uint16"), "LF": ("sbuf", [128, 128], "uint16"), "LY": ("sbuf", [128, 72], "uint16"),
+    "NS": ("sbuf", [128, 4], "int32"), "NSU": ("sbuf", [128, 2], "uint16"), "AT1": ("sbuf", [128, 112], "float32"),
+    "AR1": ("sbuf", [128, 192], "bfloat16"),
+    "W0": ("sbuf", [128, 2304], "float32"), "W1": ("sbuf", [128, 3072], "float32"),
+    "SA": ("sbuf", [128, 1152], "float32"), "EX": ("sbuf", [128, 768], "float32"),
+    "MP": ("sbuf", [128, 1152], "float32"), "YB": ("sbuf", [128, 1152], "float32"),
+    "G0": ("sbuf", [128, 2304], "float32"), "G1": ("sbuf", [128, 2304], "float32"), "G2": ("sbuf", [128, 2304], "float32"),
+    "H0": ("sbuf", [128, 2304], "float32"), "H1": ("sbuf", [128, 2304], "float32"),
+    "PT": ("psum", [128, 512], "float32"), "PM": ("psum", [128, 512], "float32"), "PS": ("psum", [128, 512], "float32"),
+    "PK": ("psum", [128, 512], "float32"), "PJ": ("psum", [128, 512], "float32"),
+    "PL0": ("psum", [128, 512], "float32"), "PL1": ("psum", [128, 512], "float32"), "PL2": ("psum", [128, 512], "float32"),
 }
-SEMAPHORES = ["left"] + ["arr%d_%d" % (t, q) for t in range(2) for q in range(4)] + ["x%d" % k for k in range(NX)]
-OWNW, SLW = 48 * 24, 16 * 24
-JOBS0 = [8, 12, 12, 16]
-JOBS1 = [8, 12, 16, 12]
-
-
-def place(q, p):
-    return OWNW + SLW * (q if q < p else q - 1)
+SEMAPHORES = ["left", "arrs", "arr0"] + ["arr1_%d" % b for b in range(3)] + ["x%d" % k for k in range(NX)]
+OWNW, SLW, BLK = 48 * 24, 16 * 24, 128 * 8
+CFG = {
+    "bv": 8,
+    "P": {"a": (0, 0, 0, 24, 2), "b": (0, 0, 24, 24, 3), "c": (0, 1, 0, 48, 2), "k": (0, 2, 0, 48, 2),
+          "d": (1, 0, 0, 48, 2), "e": (1, 1, 0, 48, 2), "f": (1, 2, 0, 20, 2), "g": (1, 2, 20, 16, 2), "h": (1, 2, 36, 12, 3)},
+    "T": "qo qa qs qk j0 j1 j2 qe q0 qy q1 q2 qj qz a1 c1 k1 d1 e1 f1 g1",
+    "S": "at ch ck as A0 A1 A2 ca bs ar ms xs an a0 b0 a1 c0 c1 k0 E0 k1 E1 E2:0:8 d0 d1 e0 e1 f0 f1 g0 g1 h0 Y:0:20 Y:20:36 Y:36:44",
+    "V": "cb cs cf id lp lh nn on rr o0 r0 bl r1 A0 cw lm A1 rn nb os A2 o1 bw ok xv nu rw nt oa le l0 uu l1 l2 lf ly "
+         "a0 b0 a1 b1 a2 c0 b2 c1 c2 k0 k1 k2 E2:8:16 d0 d1 e0 d2 e1 f0 e2 f1 g0 f2 g1 h0 g2 h1 h2 Y:44:48",
+    "stores": (0, 20, 36, 48),
+}
 
 
 def rank_program(g, core, T, topo):
@@ -55,10 +56,10 @@ def rank_program(g, core, T, topo):
     if r is None:
         return
     A, ACT = AluOpType, ActivationFunctionType
-    ops = []
+    ops, named, tag = [], {}, [None]
 
     def op(q, f, deps=(), kind="c"):
-        ops.append({"q": q, "f": f, "deps": list(deps), "kind": kind, "grp": len(ops)})
+        ops.append({"q": q, "f": f, "deps": list(deps), "kind": kind, "grp": len(ops), "tag": tag[0]})
         return len(ops) - 1
 
     def join(*ks):
@@ -80,11 +81,13 @@ def rank_program(g, core, T, topo):
     def cp(out, a, deps=()):
         return op("v", lambda: v.tensor_copy(out, a), deps)
 
-    def ac(out, a, deps=()):
-        return op("s", lambda: s.activation(out, a, ACT.Copy), deps)
+    def ac(out, a, deps=(), scale=1.0):
+        return op("s", lambda: s.activation(out, a, ACT.Copy, scale=scale), deps)
 
-    def mm(out, lhs, rhs, start, stop, deps):
-        return op("t", lambda: t.matmul(out, lhs, rhs, start, stop), deps)
+    def mms(terms, deps, first=True, last=True):
+        def mm(out, lhs, rhs, k):
+            return op("t", lambda: t.matmul(out, lhs, rhs, first and k == 0, last and k == len(terms) - 1), deps)
+        return join(*[mm(o, l, x, k) for k, (o, l, x) in enumerate(terms)])
 
     def ld(q, out, in_, deps=()):
         return op(q, lambda: queues[q].dma_start(out, in_), deps, "d")
@@ -100,248 +103,307 @@ def rank_program(g, core, T, topo):
     def bits(es):
         return sum(1 << e for e in es)
 
+    def transfer(p, srcs, dst, es, arr):
+        rid, pid = topo.addr(T.cores[p], core)
+        return RemoteDMATransfer(srcs=srcs, dsts=[dst], dst_ids=[DstId(rid=rid, pnc=pid)], dma_engine_mask=bits(es),
+                                 remote_sem=T.sem[arr], alu_op=2 if len(srcs) > 1 else 0)
+
+    left = [0]
+
+    def send(xs, engines, deps):
+        left[0] += engines
+        return op("g", lambda: g.remote_dma_fused(xs, local_sem=T.sem["left"]), deps, "r")
+
     d_ra = ld("y", T.TR[:, 0:24], T.rel[:, 0:384])
     d_po = ld("s", T.PO[:, 0:3], T.pose[:, :])
     d_rd = ld("y", T.TR[:, 24:48], T.rel[:, 192:576])
-    d_sh = ld("s", T.SHN[:, 0:4], T.shown[:, :])
+    d_sh = ld("s", T.NB[:, 12:16], T.shown[:, :])
     d_x = ld("s", T.X[:, :], T.x[:, :])
+    d_ct = join(ld("s", T.CT[:, 0:24], T.ct[:, 0:384]), ld("s", T.CT[:, 24:48], T.ct[:, 192:576]))
     d_ac = ld("s", T.AC[:, 0:3], T.act[:, :])
     d_nb = ld("s", T.NB[:, 0:12], T.nbr[:, :])
-    d_ct = join(ld("s", T.CT[:, 0:24], T.ct[:, 0:384]), ld("s", T.CT[:, 24:48], T.ct[:, 192:576]))
     join(d_ra, d_rd)
 
-    def iota(out, pat, base, cm, f32=True):
-        if f32:
+    def iota(out, pat, base, cm, flt=True):
+        if flt:
             return op("g", lambda: g.iota(out, pat, base, cm, allow_small_or_imprecise_dtypes=True))
         return op("g", lambda: g.iota(out, pat, base, cm))
 
     i_p = iota(T.IP[:, :], [[0, 2]], 0, 1, False)
     i_d = iota(T.DD[:, :], [[1, 128]], 0, -1)
     i_c = iota(T.C48[:, :], [[0, 2], [24, 48]], 0, 0)
-    i_m = iota(T.IM[:, :], [[1, 16]], 0, -1, False)
+    i_48 = iota(T.I48[:, :], [[0, 2], [1, 24]], 0, 0)
     i_g = iota(T.GI[:, :], [[1, 8], [0, 16]], 0, 0)
     i_4 = iota(T.S4[:, :], [[24, 2], [8, 2]], -48, 0)
-    i_24 = iota(T.I24[:, :], [[1, 24]], 0, 0)
-    i_n = iota(T.N4[:, :], [[48, 4]], 0, 0)
     hole = 48 + 16 * r + 16
-    i_a = [iota(T.AT[:, 0:hole], [[24, hole]], 0, 0)]
+    i_a = [iota(T.AT[:, 0:hole], [[1, hole]], 0, 0)]
     if hole < 112:
-        i_a.append(iota(T.AT[:, hole:112], [[24, 112 - hole]], 24 * (hole - 16), 0))
+        i_a.append(iota(T.AT[:, hole:112], [[1, 112 - hole]], hole - 16, 0))
     join(*i_a)
+    aeng = topo.engines(core, T.cores[near[0]])
+    send([transfer(near[0], [T.NB[:, 12 + near[0]:13 + near[0]]], T.NS[:, 0:1], aeng, "arrs")], len(aeng), [d_sh])
 
+    tag[0] = "cb"
     c_b = join(ts(T.B1[:, :], T.IP[:, :], 1, A.bitwise_and, deps=[i_p]),
                ts(T.B8[:, :], T.IP[:, :], 8, A.bitwise_and, deps=[i_p]),
                ts(T.BQ[:, :], T.IP[:, :], 15, A.bitwise_and, deps=[i_p]),
+               ts(T.B7[:, :], T.IP[:, :], 7, A.bitwise_and, deps=[i_p]),
                ts(T.BG[:, :], T.IP[:, :], 4, A.arith_shift_right, deps=[i_p]))
     c_m = join(ts(T.LO[:, :], T.B8[:, 0:1], 0, A.is_equal, deps=c_b),
                ts(T.HI[:, :], T.B8[:, 0:1], 0, A.is_gt, deps=c_b),
                ts(T.PQ[:, 0:1], T.B1[:, 0:1], 48, A.mult, deps=c_b),
                ts(T.PQ[:, 1:2], T.B1[:, 0:1], -48, A.mult, 48, A.add, deps=c_b),
                cp(T.PG[:, :], T.BG[:, 0:1], deps=c_b),
-               cp(T.QF[:, 0:1], T.BQ[:, 0:1], deps=c_b))
+               cp(T.QF[:, 0:1], T.BQ[:, 0:1], deps=c_b),
+               cp(T.QR[:, 0:1], T.B7[:, 0:1], deps=c_b))
+    tag[0] = "cs"
     c_s = join(ts(T.SH[:, :], T.DD[:, :], -8, A.is_equal, T.HI[:, :], A.mult, deps=[i_d] + c_m),
                ts(T.SL[:, :], T.DD[:, :], 8, A.is_equal, T.LO[:, :], A.mult, deps=[i_d] + c_m))
+    tag[0] = "cf"
     c_f = join(ts(T.SHW[:, :], T.DD[:, :], -8, A.is_equal, T.HI[:, :], A.mult, deps=[i_d] + c_m),
                ts(T.SLW[:, :], T.DD[:, :], 8, A.is_equal, T.LO[:, :], A.mult, deps=[i_d] + c_m))
-    im2 = ts(T.IM2[:, :], T.IM[:, :], 15, A.bitwise_and, deps=[i_m])
+    tag[0] = "id"
+    idm = ts(T.ID[:, :], T.DD[:, :], 0, A.is_equal, deps=[i_d])
+    tag[0] = "on"
     zc = op("v", lambda: v.memset(T.CW[:, 48:64], 0.0))
-    mk = ts(T.MK[:, :], T.IM2[:, :], 0, A.is_equal, deps=[im2])
     c_q = ts(T.QF[:, 1:2], T.QF[:, 0:1], 8, A.add, T.HI[:, :], A.mult, deps=c_m)
     on = ts(T.ON[:, :], T.GI[:, :], T.PG[:, :], A.is_equal, deps=[i_g] + c_m)
     sq4 = ts(T.SQ4[:, :], T.S4[:, :], T.QF[:, 0:1], A.add, deps=[i_4] + c_m)
+    tag[0] = "ch"
+    c_h = join(ac(T.SHB[:, :], T.SHW[:, :], c_f), ac(T.SLB[:, :], T.SLW[:, :], c_f), ac(T.IDB[:, :], T.ID[:, :], [idm]),
+               ac(T.LOB[:, :], T.ID[:, :], [idm] + c_m, T.LO[:, :]), ac(T.HIB[:, :], T.ID[:, :], [idm] + c_m, T.HI[:, :]))
+    tag[0] = "at"
+    i_b = ac(T.CB[:, :], T.C48[:, 0:48], [i_c])
+    i_1 = [ac(T.AT1[:, 0:48], T.AT[:, 0:48], i_a), ac(T.AT1[:, 48 + 16 * r:64 + 16 * r], T.AT[:, 0:16], i_a)]
+    for k, p in enumerate(sorted(far)):
+        i_1.append(op("s", lambda k=k, p=p: s.activation(T.AT1[:, 48 + 16 * p:64 + 16 * p], T.AT[:, 0:16], ACT.Identity, bias=96.0 + 16 * k), i_a))
+    join(*i_1)
+    tag[0] = "ck"
+    c_24 = join(ac(T.L24[:, :], T.LOB[:, :], c_h, 24.0), ac(T.H24[:, :], T.HIB[:, :], c_h, 24.0))
 
+    tag[0] = "lp"
     lp = join(*[ts(T.LP[:, 3 * k:3 * k + 3], T.PO[:, 0:3], 24 * k, A.add, deps=[d_po]) for k in range(2)])
+    tag[0] = "lh"
+    lsh = join(*[ts(T.LSH[:, 4 * k:4 * k + 4], T.NB[:, 12:16], T.PQ[:, k:k + 1], A.add, deps=c_m + [d_sh]) for k in range(2)])
+    tag[0] = "nn"
     nn = tt(T.NN[:, :], T.TR[:, :].indirect(T.LP[:, 0:6]), T.C48[:, :], A.add, deps=lp + [d_ra, d_rd, i_c])
-    shf = cp(T.SHF[:, :], T.SHN[:, :], deps=[d_sh])
-    wt = cp(T.WT[:, :], T.TR[:, :], deps=[d_ra, d_rd])
-    lsh = join(*[ts(T.LSH[:, k::3], T.PQ[:, :], T.SHF[:, p:p + 1], A.add, deps=c_m + [shf]) for k, p in enumerate(dest)])
-    rr = cp(T.RR[:, :], T.NN[:, :].indirect(T.LSH[:, 0:6]), deps=[nn] + lsh)
-    trg = ac(T.TRG[:, :], T.WT[:, :].indirect(T.LP[:, 0:6]), deps=lp + [wt])
-    idt = tt(T.IT[:, :], T.WT[:, 0:16], T.MK[:, :], A.mult, deps=[wt, mk])
-    la = [cp(T.LA[:, 0::3], T.RR[:, 0:48:2], deps=[rr]), cp(T.LA[:, 2::3], T.RR[:, 1:48:2], deps=[rr])]
-    qa = join(mm(T.PT[:, 0:24], T.SH[:, :], T.RR[:, 48:96:2], True, False, [rr] + c_s),
-              mm(T.PT[:, 0:24], T.SL[:, :], T.RR[:, 49:96:2], False, True, [rr] + c_s))
-    idc = op("v", lambda: v.tensor_reduce(T.IDC[:, :], T.IT[:, :], AxisListType.X, A.add), [idt])
-    qo = join(mm(T.PM[:, 0:24], T.SHW[:, :], T.NN[:, 48:96:2], True, False, [nn] + c_f),
-              mm(T.PM[:, 0:24], T.SLW[:, :], T.NN[:, 1:48:2], False, True, [nn] + c_f))
-    ow = [cp(T.OWN[:, 0::3], T.NN[:, 0:48:2], deps=[nn])]
-    la.append(cp(T.LA[:, 1::3], T.PT[:, 0:24], deps=qa))
+    tag[0] = "rr"
+    rr = cp(T.RR[:, :], T.NN[:, :].indirect(T.LSH[:, :]), deps=[nn] + lsh)
+    tag[0] = "as"
+    as_ = ac(T.AS[:, :], T.I48[:, :].indirect(T.LP[:, :]), deps=lp + [i_48])
+    tag[0] = "o0"
+    ow = [cp(T.OWN[:, 0::3], T.NN[:, 0:48:2], deps=[nn]), cp(T.OWN[:, 2::3], T.NN[:, 49:96:2], deps=[nn])]
+    tag[0] = "r0"
+    la = [cp(T.LA[:, 0::3], T.RR[:, 0:64:2], deps=[rr]), cp(T.LA[:, 2::3], T.RR[:, 1:64:2], deps=[rr])]
+    tag[0] = "qa"
+    qa = mms([(T.PT[:, 0:32], T.SH[:, :], T.RR[:, 64:128:2]), (T.PT[:, 0:32], T.SL[:, :], T.RR[:, 65:128:2])], [rr] + c_s)
+    tag[0] = "qo"
+    qo = mms([(T.PM[:, 0:24], T.SHW[:, :], T.NN[:, 48:96:2]), (T.PM[:, 0:24], T.SLW[:, :], T.NN[:, 1:48:2])], [nn] + c_f)
+    tag[0] = "r1"
+    la.append(cp(T.LA[:, 1::3], T.PT[:, 0:32], deps=qa))
     join(*la)
 
+    tag[0] = "bl"
     bl = join(*[ts(T.BL[:, 8 * k:8 * k + 8], T.ON[:, 0::16], T.SQ4[:, k:k + 1], A.mult, 48, A.add, deps=[on, sq4]) for k in range(4)])
-    ow.append(cp(T.OWN[:, 2::3], T.NN[:, 49:96:2], deps=[nn]))
+    tag[0] = "o1"
     ow.append(cp(T.OWN[:, 1::3], T.PM[:, 0:24], deps=qo))
     join(*ow)
+    tag[0] = "rn"
+    c_r = join(ts(T.RN[:, 0:128], T.ON[:, :], T.QF[:, 0:1], A.mult, deps=[on] + c_m),
+               ts(T.RN[:, 128:256], T.ON[:, :], T.QF[:, 1:2], A.mult, deps=[on, c_q]))
 
-    def transfer(p, srcs, win, es, arr, alu=0):
-        rid, pid = topo.addr(T.cores[p], core)
-        c = place(r, p)
-        return RemoteDMATransfer(srcs=srcs, dsts=[win[:, c:c + SLW]], dst_ids=[DstId(rid=rid, pnc=pid)],
-                                 dma_engine_mask=bits(es), remote_sem=T.sem[arr], alu_op=alu)
-
-    left = [0]
-
-    def send(p, srcs, win, arr, alu, deps):
-        es = feng if p in far else neng
-        left[0] += len(es)
-        x = transfer(p, srcs, win, es, arr, alu)
-        return op("g", lambda: g.remote_dma_fused([x], local_sem=T.sem["left"]), deps, "r")
+    def slot(p):
+        return r if r < p else r - 1
 
     for k, p in enumerate(dest):
         a, b = SLW * k, SLW * k + SLW // 2
-        x = join(cp(T.SA[:, a:b], T.X[:, :].indirect(T.LA[:, 24 * k:24 * k + 12]), deps=la + [d_x]),
-                 ac(T.SA[:, b:a + SLW], T.X[:, :].indirect(T.LA[:, 24 * k + 12:24 * k + 24]), deps=la + [d_x]))
-        send(p, [T.SA[:, a:a + SLW]], T.W0, "arr0_%d" % r, 0, x)
-    arr0, arr1 = [[("sem", "arr%d_%d" % (k, q), len(feng) if q in far else len(neng)) for q in others] for k in range(2)]
+        tag[0] = "A%d" % k
+        x = join(cp(T.SA[:, a:b], T.X[:, :].indirect(T.LA[:, 24 * p:24 * p + 12]), deps=la + [d_x]),
+                 ac(T.SA[:, b:a + SLW], T.X[:, :].indirect(T.LA[:, 24 * p + 12:24 * p + 24]), deps=la + [d_x]))
+        c, es = OWNW + SLW * slot(p), feng if p in far else neng
+        send([transfer(p, [T.SA[:, a:a + SLW]], T.W0[:, c:c + SLW], es, "arr0")], len(es), x)
+    arr0 = [("sem", "arr0", 2 * len(feng) + len(neng))]
+    half = len(feng) // 2
+    eng1 = {far[0]: feng[:half], far[1]: feng[half:]}
+    arr1 = [[("sem", "arr1_%d" % b, len(feng) + len(neng))] for b in range(3)]
 
-    lm = join(*[cp(T.LM[:, 3 * k:3 * k + 3], T.AC[:, 0:3], deps=[d_ac]) for k in range(2)])
-    cw = join(cp(T.CW[:, 0:24], T.CT[:, 0:24], deps=d_ct), ts(T.CW[:, 24:48], T.CT[:, 24:48], T.HI[:, :], A.mult, deps=d_ct + c_m))
-    ms = ac(T.MS[:, :], T.I24[:, :].indirect(T.LM[:, :]), deps=lm + [i_24])
-    nbu = cp(T.NBU[:, :], T.NB[:, :], deps=[d_nb])
-    bd = join(ac(T.BD[:, 0:256], T.CW[:, :].indirect(T.BL[:, 0:16]), deps=bl + cw + [zc]),
-              cp(T.BD[:, 256:512], T.CW[:, :].indirect(T.BL[:, 16:32]), deps=bl + cw + [zc]))
-    oa = tt(T.OA[:, :], T.TRG[:, :], T.MS[:, :], A.is_equal, deps=[trg, ms])
-    arm = ac(T.ARM[:, :], T.AT[:, :].indirect(T.NBU[:, :]), deps=i_a + [nbu])
+    even0, odd0, even1, odd1 = [slice(k, k - k % 2 + 48, 2) for k in (0, 1, 48, 49)]
+    picks = [((T.LOB, even0), (T.SLB, odd0)), ((T.LOB, even1), (T.HIB, odd0)), ((T.SHB, even1), (T.HIB, odd1))]
+    bv = CFG["bv"]
 
     def rows(out, oh, deps):
-        return join(*[mm(out[:, 48 * h:48 * h + 48], T.BD[:, 256 * k + 128 * h:256 * k + 128 * h + 128], oh[:, 48 * k:48 * k + 48],
-                         k == 0, k == 1, deps) for h in range(2) for k in range(2)])
+        return join(*sum([mms([(out[:, 48 * h:48 * h + 48], T.BD[:, 256 * k + 128 * h:256 * k + 128 * h + 128], oh[:, 48 * k:48 * k + 48])
+                               for k in range(2)], deps) for h in range(2)], []))
 
-    def plus(out, P, deps):
-        return join(*[tt(out[:, 192 * h + 48 * n:192 * h + 48 * n + 48], T.ARM[:, 48 * n:48 * n + 48], P[:, 48 * h:48 * h + 48], A.add, deps)
-                      for h in range(2) for n in range(4)])
 
-    def middle(P, up, down, even, odd, deps):
-        return join(mm(P, up, even, True, False, deps), mm(P, down, odd, False, True, deps))
+    def natural():
+        parts = [T.UU[:, 96 * k:96 * k + 96] for k in range(3)]
+        P, d = T.PM, ["uu"] + ow + c_h + [i_b]
+        return join(*(
+            mms([(P[:, 0:24], T.IDB[:, :], T.CB[:, even0])] + [(P[:, 0:24], T.IDB[:, :], x[:, even0]) for x in parts], d) +
+            mms([(P[:, 24:48], T.LOB[:, :], T.CB[:, even0]), (P[:, 24:48], T.HIB[:, :], T.CB[:, odd0])] +
+                [(P[:, 24:48], T.SHB[:, :], x[:, even1]) for x in parts] + [(P[:, 24:48], T.SLB[:, :], x[:, odd0]) for x in parts], d) +
+            mms([(P[:, 48:72], T.IDB[:, :], T.CB[:, odd0])] + [(P[:, 48:72], T.IDB[:, :], x[:, odd1]) for x in parts], d)))
 
-    qy = rows(T.PY, T.OA, [oa] + bd)
-    c_r = join(ts(T.RN[:, 0:128], T.ON[:, :], T.QF[:, 0:1], A.mult, deps=[on] + c_m),
-               ts(T.RN[:, 128:256], T.ON[:, :], T.QF[:, 1:2], A.mult, deps=[on, c_q]))
-    c_p = ts(T.PQ4[:, :], T.PQ[:, :], 4, A.mult, deps=c_m)
-    idm = ts(T.ID[:, :], T.DD[:, :], 0, A.is_equal, deps=[i_d])
-    c_np = join(ts(T.NP[:, :], T.N4[:, :], T.PQ4[:, 0:1], A.add, deps=[i_n, c_p]),
-                ts(T.NM[:, :], T.N4[:, :], T.PQ4[:, 1:2], A.add, deps=[i_n, c_p]))
-    own0 = [ac(T.W0[:, 0:OWNW], T.X[:, :].indirect(T.OWN[:, :]), deps=ow + [d_x])]
-    ov = ts(T.OV[:, :], T.PY[:, 0:96], T.IDC[:, :], A.is_equal, deps=qy + [idc])
-    qv = join(*[mm(T.PV[:, 48 * h:48 * h + 48], T.RN[:, 128 * k:128 * k + 128], T.OV[:, 48 * k:48 * k + 48], k == 0, k == 1, [ov] + c_r)
-                for h in range(2) for k in range(2)])
-    zy = plus(T.ZY, T.PY, qy + [arm])
-    ok = tt(T.OK[:, :], T.TRG[:, :], T.PV[:, 0:96], A.is_equal, deps=qv + [trg])
-    qk = rows(T.PK, T.OK, [ok] + bd)
-    ls = join(*([ts(T.LS2[:, 4 * k:4 * k + 4], T.NM[:, :], T.SHF[:, p:p + 1], A.add, deps=c_np + [shf]) for k, p in enumerate(dest)] +
-                [ts(T.LS1[:, 4 * k:4 * k + 4], T.NP[:, :], T.SHF[:, p:p + 1], A.add, deps=c_np + [shf]) for k, p in enumerate(dest)]))
-    qz = middle(T.PV[:, 0:96], T.SHW[:, :], T.SLW[:, :], T.ZY[:, 192:384:2], T.ZY[:, 1:192:2], zy + c_f + [ok])
-    ly = [cp(T.LY[:, 0::3], T.ZY[:, 0:192:2], deps=zy)]
-    z = plus(T.Z, T.PK, qk + [arm])
-    ly.append(cp(T.LY[:, 2::3], T.ZY[:, 193:384:2], deps=zy))
-    zs2 = ts(T.ZS2[:, :], T.Z[:, :].indirect(T.LS2[:, :]), -OWNW, A.add, deps=z + ls)
-    zs1 = ac(T.ZS1[:, :], T.Z[:, :].indirect(T.LS1[:, :]), deps=z + ls)
-    qb = middle(T.PM[:, 0:96], T.SH[:, :], T.SL[:, :], T.ZS2[:, 0::2], T.ZS2[:, 1::2], [zs2] + c_s + ow)
-    qc = middle(T.PT[:, 0:96], T.SHW[:, :], T.SLW[:, :], T.Z[:, 192:384:2], T.Z[:, 1:192:2], z + c_f + la)
-    ly.append(cp(T.LY[:, 1::3], T.PV[:, 0:96], deps=qz))
-    join(*ly)
-    lc = [cp(T.LC[:, 0::3], T.Z[:, 0:192:2], deps=z), cp(T.LC[:, 2::3], T.Z[:, 193:384:2], deps=z)]
-    lb = join(ts(T.LB[:, 1::3], T.PM[:, 0:96], OWNW, A.add, deps=qb),
-              cp(T.LB[:, 0::3], T.ZS1[:, 0::2], deps=[zs1]), cp(T.LB[:, 2::3], T.ZS1[:, 1::2], deps=[zs1]))
+    step = {
+        "cw": lambda: join(cp(T.CW[:, 0:24], T.CT[:, 0:24], deps=d_ct),
+                           ts(T.CW[:, 24:48], T.CT[:, 24:48], T.HI[:, :], A.mult, deps=d_ct + c_m)),
+        "lm": lambda: join(*[ts(T.LM[:, 3 * k:3 * k + 3], T.AC[:, 0:3], 24 * k, A.add, deps=[d_ac]) for k in range(2)]),
+        "nb": lambda: [cp(T.NBU[:, :], T.NB[:, :], deps=[d_nb, d_sh])],
+        "os": lambda: [tt(T.OS[:, :], T.CW[:, :].indirect(T.LM[:, :]), T.AS[:, :], A.is_equal, deps=["cw", "lm", as_, zc])],
+        "ca": lambda: [ac(T.CA[:, :], T.CW[:, :].indirect(T.LP[:, :]), deps=lp + ["cw", zc])],
+        "bs": lambda: [ac(T.BD[:, 0:256], T.CW[:, :].indirect(T.BL[:, 0:16]), deps=bl + ["cw", zc])],
+        "bw": lambda: [cp(T.BD[:, 256:512], T.CW[:, :].indirect(T.BL[:, 16:32]), deps=bl + ["cw", zc])],
+        "ar": lambda: [ac(T.ARM[:, :], T.AT[:, :].indirect(T.NBU[:, :]), deps=i_a + ["nb"])],
+        "qs": lambda: join(*sum([mms([(T.PS[:, 48 * h:48 * h + 48], T.RN[:, 128 * k:128 * k + 128], T.OS[:, 48 * k:48 * k + 48])
+                                      for k in range(2)], ["os"] + c_r) for h in range(2)], [])),
+        "ok": lambda: [tt(T.OK[:, :], T.CA[:, :], T.PS[:, 0:96], A.is_equal, deps=["qs", "ca"])],
+        "qk": lambda: rows(T.PK, T.OK, ["ok", "bs", "bw"]),
+        "rw": lambda: [cp(T.RW[:, :], T.PK[:, 0:96], deps=["qk"])],
+        "qe": lambda: join(*sum([mms([(T.PJ[:, 8 * k:8 * k + 8], m[:, :], T.ARM[:, 192 + 16 * p + h:208 + 16 * p:2])
+                                      for h, m in enumerate((T.LOB, T.HIB))], ["ar"] + c_h) for k, p in enumerate(sorted(far))], [])),
+        "le": lambda: [ts(T.LF[:, 96:112], T.PJ[:, 0:16], 8, A.mult, T.QR[:, :], A.add, deps=["qe"] + c_m)],
+        "nu": lambda: [cp(T.NSU[:, 0:1], T.NS[:, 0:1], deps=[("sem", "arrs", len(aeng))])],
+        "nt": lambda: [ts(T.AT1[:, 48 + 16 * near[0]:64 + 16 * near[0]], T.AT[:, 0:48].indirect(T.NSU[:, 0:1]), 48, A.add, deps=i_a + ["nu"])],
+        "an": lambda: [ac(T.AR1[:, :], T.AT1[:, :].indirect(T.NBU[:, 0:12]), deps=i_1 + ["nb", "nt"])],
+        "qj": lambda: mms([(T.PJ[:, 0:96], T.LOB[:, :], T.AR1[:, 0::2]), (T.PJ[:, 0:96], T.HIB[:, :], T.AR1[:, 1::2])], ["an", "le"] + c_h),
+        "lf": lambda: [ts(T.LF[:, 0:96], T.PJ[:, 0:96], 8, A.mult, T.QR[:, :], A.add, deps=["qj"] + c_m)],
+        "xs": lambda: [ac(T.W0[:, 24 * bv:OWNW], T.X[:, :].indirect(T.OWN[:, bv * 3 // 2:72]), deps=ow + [d_x])],
+        "xv": lambda: [cp(T.W0[:, 0:24 * bv], T.X[:, :].indirect(T.OWN[:, 0:bv * 3 // 2]), deps=ow + [d_x])] if bv else [],
+        "ms": lambda: [ac(T.MS[:, :], T.I48[:, :].indirect(T.LM[:, :]), deps=["lm", i_48])],
+        "oa": lambda: [tt(T.OA[:, :], T.TR[:, :].indirect(T.LP[:, :]), T.MS[:, :], A.is_equal, deps=["ms"])],
+        "qy": lambda: rows(T.PT, T.OA, ["oa", "bs", "bw"] + la),
+        "uu": lambda: join(ts(T.UU[:, 0:96], T.PT[:, 0:96], 3, A.mult, deps=["qy"]),
+                           ts(T.UU[:, 96:192], T.PT[:, 0:96], 8, A.is_ge, -23, A.mult, deps=["qy"]),
+                           ts(T.UU[:, 192:288], T.PT[:, 0:96], 16, A.is_ge, -23, A.mult, deps=["qy"])),
+        "qz": natural,
+        "ly": lambda: join(*[cp(T.LY[:, k::3], T.PM[:, 24 * k:24 * k + 24], deps=["qz"]) for k in range(3)]),
+    }
+    for b in range(3):
+        step["j%d" % b] = lambda b=b: mms([(T["PL%d" % b][:, 0:96], m[:, :], T.ARM[:, h:192:2]) for h, m in enumerate((T.L24, T.H24))],
+                                          ["ar"] + c_24, last=False)
+        step["q%d" % b] = lambda b=b: mms([(T["PL%d" % b][:, 24 * n:24 * n + 24], m[:, :], T.RW[:, c]) for n in range(4) for m, c in picks[b]],
+                                          ["rw"] + c_h, first=False)
+        step["l%d" % b] = lambda b=b: [cp(T.LC[:, 96 * b:96 * b + 96], T["PL%d" % b][:, 0:96], deps=["q%d" % b])]
 
-    for k, p in enumerate(dest):
-        lists = [T.LB[:, 96 * k + 24 * n:96 * k + 24 * n + 24] for n in range(4)]
-        f0, f1, f2, f3 = [T[x][:, SLW * k:SLW * k + SLW] for x in ("F0", "F1", "F2", "F3")]
-        deps = lb + own0 + arr0
-        if k == 2:
-            lc.append(cp(T.LC[:, 1::3], T.PT[:, 0:96], deps=qc))
-            join(*lc)
-        hw = SLW // 2
-        x0 = [cp(f0[:, hw * h:hw * h + hw], T.W0[:, :].indirect(lists[0][:, 12 * h:12 * h + 12]), deps) for h in range(2)]
-        x1 = [tt(f1[:, hw * h:hw * h + hw], T.W0[:, :].indirect(lists[1][:, 12 * h:12 * h + 12]), f0[:, hw * h:hw * h + hw], A.max,
-                 deps + [x0[h]]) for h in range(2)]
-        x = join(*x1, ac(f2, T.W0[:, :].indirect(lists[2]), deps), ac(f3, T.W0[:, :].indirect(lists[3]), deps))
-        send(p, [f1, f2, f3], T.W1, "arr1_%d" % r, 2, x)
-
-    banks = [[T.PC0, []], [T.PC1, []], [T.PC2, []], [T.PM, lb], [T.PT, lc], [T.PK, z], [T.PV, ly], [T.PY, zy]]
-    spare, turn = [0], [0]
-
-    def pieces(win, lists, jobs, deps, out, stored):
-        js, at = [], 0
-        for nodes in jobs:
-            w, c = nodes * 24, spare[0]
-            src = [win[:, :].indirect(lists[:, 72 * n + at // 2 * 3:72 * n + (at + nodes) // 2 * 3]) for n in range(4)]
-            js.append({"w": w, "src": src, "out": out[:, at * 24:(at + nodes) * 24]})
-            js[-1].update({x: T[x][:, c:c + w] for x in ("G2", "G3", "H0", "H1", "H2")})
-            spare[0] += w
-            at += nodes
-
-        def third(j):
-            g3 = ac(j["G3"], j["src"][3], deps)
-            bank = banks[turn[0] % len(banks)]
-            turn[0] += 1
-            j["P"] = bank[0][:, 0:j["w"]]
-            if j is js[-1]:
-                j["p"] = ac(j["P"], j["G3"], [g3] + bank[1])
-            else:
-                j["p"] = mm(j["P"], T.ID[:, :], j["G3"], True, True, [g3, idm] + bank[1])
-            j["bank"] = bank
-        for k, j in enumerate(js[1:]):
-            j["g"] = ac(j["G2"], j["src"][2], deps)
-            if k == 0:
-                third(js[0])
-            third(j)
-
-        res = []
-
-        def first(j):
-            j["h"] = tt(j["H1"], j["src"][0], j["G2"], A.max, deps + [j["g"]])
-
-        def second(j):
-            j["h"] = tt(j["H2"], j["src"][2 if j is js[0] else 1], j["H1"], A.max, deps + [j["h"]])
-
-        def last(k):
-            j = js[k]
-            e = tt(j["out"], j["H2"], j["P"], A.max, [j["h"], j["p"]])
-            j["bank"][1] = [e]
-            res.append(e)
-            if stored:
-                stored(k, e)
-        h = cp(js[0]["H0"], js[0]["src"][0], deps)
-        js[0]["h"] = tt(js[0]["H1"], js[0]["src"][1], js[0]["H0"], A.max, deps + [h])
-        first(js[1])
-        second(js[0])
-        n = len(js)
-        if stored:
-            second(js[1])
-            last(0)
-            for k in range(2, n):
-                first(js[k])
-                last(k - 1)
-                second(js[k])
+    banks = [[T.PS, ["ok"]], [T.PK, ["rw"]], [T.PL0, ["l0"]], [T.PL1, ["l1"]], [T.PL2, ["l2"]], [T.PJ, ["lf"]]]
+    turn = [0]
+    own0 = ["xs", "xv"]
+    P = {}
+    at = 0
+    for k, (rd, b, i0, n, kv) in CFG["P"].items():
+        w = 8 * n
+        j = {"rd": rd, "b": b, "i0": i0, "n": n, "kv": kv, "w": w}
+        if rd == 0:
+            win, lst, c0 = T.W0[:, :], T.LC, 96 * b
+            j["deps"], j["out"] = ["l%d" % b] + own0 + arr0, T.W1[:, BLK * b + 8 * i0:BLK * b + 8 * (i0 + n)]
         else:
-            for k in range(2, n):
-                first(js[k])
-                second(js[k - 1])
-                last(k - 2)
-            second(js[n - 1])
-            last(n - 2)
-        last(n - 1)
-        return res
+            win, lst, c0 = T.W1[:, BLK * b:BLK * b + BLK], T.LF, 0
+            j["deps"], j["out"] = ["lf", "W%d" % b] + arr1[b], T.MP[:, 24 * i0 + b:24 * (i0 + n):3]
+        j.update({"win": win, "lst": lst, "c0": c0 + i0 // 2, "at": at})
+        j["src"] = [win.indirect(lst[:, j["c0"] + 24 * m:j["c0"] + 24 * m + n // 2]) for m in range(4)]
+        j["G"] = T.G0[:, at:at + w]
+        j["H"] = [T["H%d" % m][:, at:at + w] for m in range(2)]
+        at += w
+        P[k] = j
 
-    own1 = pieces(T.W0, T.LC, JOBS0, lc + own0 + arr0, T.W1, None)
+    def scalar_step(ks, m):
+        j, w = P[ks[0]], sum(P[k]["w"] for k in ks)
+        c = j["c0"] + 24 * (3 - m)
+        x = ac(T["G%d" % m][:, j["at"]:j["at"] + w], j["win"].indirect(j["lst"][:, c:c + w // 16]), j["deps"])
+        for k in ks:
+            named[k + ("g0" if m == 0 else "s%d" % m)] = [x]
 
+    def tensor_step(ks, m):
+        j, w = P[ks[0]], sum(P[k]["w"] for k in ks)
+        bank = banks[turn[0] % len(banks)]
+        turn[0] += 1
+        x = mms([(bank[0][:, 0:w], T.ID[:, :], T["G%d" % m][:, j["at"]:j["at"] + w])], [k + "s%d" % m for k in ks] + [idm] + bank[1])
+        for k in ks:
+            c = P[k]["at"] - j["at"]
+            P[k]["P%d" % m], named[k + "g%d" % m] = bank[0][:, c:c + P[k]["w"]], x
+        bank[1] = [k + "v%d" % (P[k]["kv"] + m - 1) for k in ks]
+
+    def vector_step(k, m):
+        j = P[k]
+        kv = j["kv"]
+        out = j["out"] if m == 2 else j["H"][m]
+        prev = (j["G"], k + "g0") if m == 0 else (j["H"][m - 1], k + "v%d" % (m - 1))
+        if m < kv:
+            x = tt(out, j["src"][m], prev[0], A.max, j["deps"] + [prev[1]])
+        else:
+            u = m - kv + 1
+            x = tt(out, prev[0], j["P%d" % u], A.max, [prev[1], k + "g%d" % u])
+        named[k + "v%d" % m] = [x]
+        if m == 2:
+            named.setdefault(("W%d" if j["rd"] == 0 else "M%d") % j["b"], []).append(x)
+            named[k + "done"] = [x]
+
+    def shown(b, q, lo, hi):
+        f = ac if q == "s" else cp
+        named.setdefault("E%d" % b, []).append(
+            f(T.EX[:, 256 * b + 16 * lo:256 * b + 16 * hi], T.W1[:, BLK * b:BLK * b + 384].indirect(T.LF[:, 96 + lo:96 + hi]), ["le", "W%d" % b]))
+
+    finals = []
+
+    def final(q, a, b):
+        f = ac if q == "s" else cp
+        finals.append((a, b, f(T.YB[:, 24 * a:24 * b], T.MP[:, 0:24 * b].indirect(T.LY[:, a * 3 // 2:b * 3 // 2]),
+                               ["ly"] + [x + "done" for x in P if P[x]["rd"] == 1 and P[x]["i0"] < b])))
+
+    early = set(o["tag"] for o in ops)
+    for q in "tsv":
+        for w in CFG[q.upper()].split():
+            tag[0] = w
+            w, lo, hi = (w.split(":") + [0, 48])[:3]
+            if w in early:
+                continue
+            if w[0] == "E":
+                shown(int(w[1]), q, int(lo), min(int(hi), 16))
+            elif w[0] == "Y":
+                final(q, int(lo), int(hi))
+            elif w in step:
+                named[w] = step[w]()
+            elif q == "t":
+                tensor_step(w[:-1], int(w[-1]))
+            elif q == "s":
+                scalar_step(w[:-1], int(w[-1]))
+            else:
+                vector_step(w[0], int(w[1]))
+
+    for b in range(3):
+        c = BLK * b
+        send([transfer(near[0], [T.W1[:, c:c + 384]], T.W1[:, c + 384:c + 768], neng, "arr1_%d" % b)], len(neng), ["W%d" % b])
+        c += 768 + 128 * sorted([r] + near).index(r)
+        send([transfer(p, [T.EX[:, 256 * b + 128 * k:256 * b + 128 * k + 128]], T.W1[:, c:c + 128], eng1[p], "arr1_%d" % b)
+              for k, p in enumerate(sorted(far))], len(feng), ["E%d" % b])
     stores = []
-
-    def store(k, m):
-        a, b = sum(JOBS1[:k]) * 24, sum(JOBS1[:k + 1]) * 24
-        stores.append(ld("y", T.y[:, a:b], T.YB[:, a:b], [m]))
-
-    pieces(T.W1, T.LY, JOBS1, ly + own1 + arr1, T.YB, store)
+    for a, b in zip(CFG["stores"], CFG["stores"][1:]):
+        stores.append(ld("y", T.y[:, 24 * a:24 * b], T.YB[:, 24 * a:24 * b], [x for lo, hi, x in finals if lo < b and a < hi]))
     op("y", None, stores, "w")
     op("g", None, [("sem", "left", left[0])], "w")
 
+    for o in ops:
+        o["deps"] = sum([named[d] if isinstance(d, str) else [d] for d in o["deps"]], [])
     used, total = set(), {}
     for o in ops:
         used.update(ops[d]["grp"] for d in o["deps"] if not isinstance(d, tuple))
     for o in ops:
         total[o["grp"]] = total.get(o["grp"], 0) + (16 if o["kind"] == "d" else 1)
-    names = {k: "x%d" % n for n, k in enumerate(sorted(used))}
+    order = {q: CFG.get(q.upper(), "").split() for q in queues}
+    seq = sorted(ops, key=lambda o: order[o["q"]].index(o["tag"]) if o["q"] in "vst" and o["kind"] == "c" else -1)
+    seen, before = {q: set() for q in queues}, {}
+    for o in seq:
+        seen[o["q"]].update(ops[d]["grp"] for d in o["deps"] if not isinstance(d, tuple) and ops[d]["kind"] == "c")
+        before[o["grp"]] = before.get(o["grp"], seen[o["q"]]) & seen[o["q"]]
+    names, taken, spare = {}, set(), len(used) - NX
+    for k in sorted(used):
+        free = sorted(a for a in before[k] if a in names and a not in taken)
+        if spare > 0 and free and ops[k]["kind"] == "c":
+            taken.add(free[0])
+            names[k], total[k], spare = names[free[0]], total[k] + total[free[0]], spare - 1
+        else:
+            names[k] = "x%d" % len(set(names.values()))
     done = {q: {} for q in queues}
 
     def wait(q, name, val):
@@ -349,7 +411,7 @@ def rank_program(g, core, T, topo):
             queues[q].wait_ge(T.sem[name], val)
             done[q][name] = val
 
-    for o in ops:
+    for o in seq:
         for d in o["deps"]:
             if isinstance(d, tuple):
                 wait(o["q"], d[1], d[2])

@@ -5,11 +5,13 @@ NX = 144
 SCRATCH = {
     "X": ("sbuf", [128, 1152], "float32"), "TR": ("sbuf", [128, 48], "int32"), "PO": ("sbuf", [128, 4], "int32"),
     "NB": ("sbuf", [128, 16], "int32"), "AC": ("sbuf", [128, 4], "int32"), "CT": ("sbuf", [128, 48], "int32"),
+    "NS": ("sbuf", [128, 4], "int32"),
     "IP": ("sbuf", [128, 2], "int32"), "DD": ("sbuf", [128, 128], "float32"), "GI": ("sbuf", [128, 128], "float32"),
     "C48": ("sbuf", [128, 96], "float32"), "CB": ("sbuf", [128, 48], "bfloat16"), "S4": ("sbuf", [128, 4], "float32"),
     "SQ4": ("sbuf", [128, 4], "float32"), "AT": ("sbuf", [128, 112], "float32"), "I48": ("sbuf", [128, 48], "float32"),
-    "B1": ("sbuf", [128, 2], "int32"), "B8": ("sbuf", [128, 2], "int32"), "BQ": ("sbuf", [128, 2], "int32"),
-    "B7": ("sbuf", [128, 2], "int32"), "QR": ("sbuf", [128, 1], "float32"),
+    "AT1": ("sbuf", [128, 112], "float32"),
+    "B1": ("sbuf", [128, 2], "int32"), "BQ": ("sbuf", [128, 2], "int32"),
+    "B7": ("sbuf", [128, 2], "int32"), "QR": ("sbuf", [128, 1], "float32"), "PF": ("sbuf", [128, 1], "float32"),
     "BG": ("sbuf", [128, 2], "int32"), "PG": ("sbuf", [128, 1], "float32"), "QF": ("sbuf", [128, 2], "float32"),
     "LO": ("sbuf", [128, 1], "float32"), "HI": ("sbuf", [128, 1], "float32"), "PQ": ("sbuf", [128, 2], "float32"),
     "SH": ("sbuf", [128, 128], "float16"), "SL": ("sbuf", [128, 128], "float16"), "ON": ("sbuf", [128, 128], "bfloat16"),
@@ -24,13 +26,14 @@ SCRATCH = {
     "NBU": ("sbuf", [128, 16], "uint16"), "CW": ("sbuf", [128, 64], "float32"), "BD": ("sbuf", [128, 512], "bfloat16"),
     "AS": ("sbuf", [128, 96], "float32"), "MS": ("sbuf", [128, 96], "float32"), "CA": ("sbuf", [128, 96], "float32"),
     "OA": ("sbuf", [128, 96], "bfloat16"), "OS": ("sbuf", [128, 96], "bfloat16"), "OK": ("sbuf", [128, 96], "bfloat16"),
-    "ARM": ("sbuf", [128, 256], "bfloat16"), "RW": ("sbuf", [128, 96], "bfloat16"), "UU": ("sbuf", [128, 288], "bfloat16"),
-    "LC": ("sbuf", [128, 288], "uint16"), "LF": ("sbuf", [128, 128], "uint16"), "LY": ("sbuf", [128, 72], "uint16"),
-    "NS": ("sbuf", [128, 4], "int32"), "NSU": ("sbuf", [128, 2], "uint16"), "AT1": ("sbuf", [128, 112], "float32"),
-    "AR1": ("sbuf", [128, 192], "bfloat16"),
+    "ARM": ("sbuf", [128, 256], "bfloat16"), "RW": ("sbuf", [128, 96], "bfloat16"),
+    "UU": ("sbuf", [128, 288], "bfloat16"), "UD": ("sbuf", [128, 288], "bfloat16"),
+    "AR1": ("sbuf", [128, 192], "bfloat16"), "NSU": ("sbuf", [128, 2], "uint16"),
+    "LC": ("sbuf", [128, 288], "uint16"), "LF": ("sbuf", [128, 96], "uint16"), "LE": ("sbuf", [128, 16], "uint16"),
+    "LY": ("sbuf", [128, 72], "uint16"), "LD": ("sbuf", [128, 72], "uint16"),
     "W0": ("sbuf", [128, 2304], "float32"), "W1": ("sbuf", [128, 3072], "float32"),
-    "SA": ("sbuf", [128, 1152], "float32"), "EX": ("sbuf", [128, 768], "float32"),
-    "MP": ("sbuf", [128, 1152], "float32"), "YB": ("sbuf", [128, 1152], "float32"),
+    "SA": ("sbuf", [128, 1152], "float32"), "EX": ("sbuf", [128, 768], "float32"), "EG": ("sbuf", [128, 768], "float32"),
+    "MP": ("sbuf", [128, 1152], "float32"), "YB": ("sbuf", [128, 1152], "float32"), "DB": ("sbuf", [128, 1152], "float32"),
     "G0": ("sbuf", [128, 2304], "float32"), "G1": ("sbuf", [128, 2304], "float32"), "G2": ("sbuf", [128, 2304], "float32"),
     "H0": ("sbuf", [128, 2304], "float32"), "H1": ("sbuf", [128, 2304], "float32"),
     "PT": ("psum", [128, 512], "float32"), "PM": ("psum", [128, 512], "float32"), "PS": ("psum", [128, 512], "float32"),
@@ -40,14 +43,16 @@ SCRATCH = {
 SEMAPHORES = ["left", "arrs", "arr0"] + ["arr1_%d" % b for b in range(3)] + ["x%d" % k for k in range(NX)]
 OWNW, SLW, BLK = 48 * 24, 16 * 24, 128 * 8
 CFG = {
-    "bv": 8,
-    "P": {"a": (0, 0, 0, 24, 2), "b": (0, 0, 24, 24, 3), "c": (0, 1, 0, 48, 2), "k": (0, 2, 0, 48, 2),
-          "d": (1, 0, 0, 48, 2), "e": (1, 1, 0, 48, 2), "f": (1, 2, 0, 20, 2), "g": (1, 2, 20, 16, 2), "h": (1, 2, 36, 12, 3)},
-    "T": "qo qa qs qk j0 j1 j2 qe q0 qy q1 q2 qj qz a1 c1 k1 d1 e1 f1 g1",
-    "S": "at ch ck as A0 A1 A2 ca bs ar ms xs an a0 b0 a1 c0 c1 k0 E0 k1 E1 E2:0:8 d0 d1 e0 e1 f0 f1 g0 g1 h0 Y:0:20 Y:20:36 Y:36:44",
-    "V": "cb cs cf id lp lh nn on rr o0 r0 bl r1 A0 cw lm A1 rn nb os A2 o1 bw ok xv nu rw nt oa le l0 uu l1 l2 lf ly "
-         "a0 b0 a1 b1 a2 c0 b2 c1 c2 k0 k1 k2 E2:8:16 d0 d1 e0 d2 e1 f0 e2 f1 g0 f2 g1 h0 g2 h1 h2 Y:44:48",
-    "stores": (0, 20, 36, 48),
+    "bv": 12, "four": 32, "G": "n0 f0 n1 f1 f2 n2", "e8": 1, "loads": "ra:y sh:s po:s rd:y x:s c0:s c1:s ac:s nb:s",
+    "P": {"a": (0, 0, 0, 24, 2), "b": (0, 0, 24, 24, 2), "c": (0, 1, 0, 48, 2), "d": (0, 2, 0, 48, 2),
+          "e": (1, 0, 0, 32, 2), "f": (1, 0, 32, 16, 2), "g": (1, 1, 0, 32, 2), "h": (1, 1, 32, 16, 2),
+          "i": (1, 2, 0, 16, 2), "k": (1, 2, 16, 16, 2), "m": (1, 2, 32, 16, 2)},
+    "T": "qa qo qs qk j1 j0 qe qy q0 j2 q1 q2 qj a1 b1 c1 qz qd d1 e1 g1 i1 k1",
+    "S": "ia as at ch A0 A1 A2 ca ms ck bs ar xs an ra a0 b0 a1 b1 c0 c1 E0 d0 d1 E1 F2 e0 f0 e1 g0 h0 g1 i0 i1 k0 m0 k1 "
+         "D:32:48 Y:0:16 Y:16:32",
+    "V": "cb cx cm cy cs lh lp id nn cf rr on r0 r1 A0 A1 lm cw A2 rn bl oa nb os nu o1 bw ok nt rw xv l0 l2 l1 le "
+         "a0 b0 a1 b1 uu a2 b2 c0 ud c1 lf c2 d0 ly d1 ld F2 d2 e0 f0 e1 f1 e2 g0 h0 g1 i0 g2 i1 k0 i2 k1 m0 k2 h1 m1 Z:32:48",
+    "stores": (0, 16, 32, 48),
 }
 
 
@@ -81,8 +86,10 @@ def rank_program(g, core, T, topo):
     def cp(out, a, deps=()):
         return op("v", lambda: v.tensor_copy(out, a), deps)
 
-    def ac(out, a, deps=(), scale=1.0):
-        return op("s", lambda: s.activation(out, a, ACT.Copy, scale=scale), deps)
+    def ac(out, a, deps=(), scale=1.0, bias=None):
+        if bias is None:
+            return op("s", lambda: s.activation(out, a, ACT.Copy, scale=scale), deps)
+        return op("s", lambda: s.activation(out, a, ACT.Identity, bias=bias, scale=scale), deps)
 
     def mms(terms, deps, first=True, last=True):
         def mm(out, lhs, rhs, k):
@@ -96,17 +103,16 @@ def rank_program(g, core, T, topo):
     near = [p for p in others if T.cores[p] in topo.cores_of(core)]
     far = [p for p in others if p not in near]
     far.sort(key=lambda p: topo.die(T.cores[p]) != topo.die(core))
-    dest = far + near
+    dest = far[:1] + near + far[1:] if CFG.get("e8") == 1 else far + near
     feng = topo.engines(core, T.cores[far[0]])
-    neng = [e for e in topo.engines(core, T.cores[near[0]]) if e not in feng]
+    aeng = topo.engines(core, T.cores[near[0]])
+    neng = [e for e in aeng if e not in feng]
+    aeng = feng if CFG.get("e8") else aeng
 
-    def bits(es):
-        return sum(1 << e for e in es)
-
-    def transfer(p, srcs, dst, es, arr):
+    def transfer(p, src, dst, es, arr):
         rid, pid = topo.addr(T.cores[p], core)
-        return RemoteDMATransfer(srcs=srcs, dsts=[dst], dst_ids=[DstId(rid=rid, pnc=pid)], dma_engine_mask=bits(es),
-                                 remote_sem=T.sem[arr], alu_op=2 if len(srcs) > 1 else 0)
+        return RemoteDMATransfer(srcs=[src], dsts=[dst], dst_ids=[DstId(rid=rid, pnc=pid)], dma_engine_mask=sum(1 << e for e in es),
+                                 remote_sem=T.sem[arr])
 
     left = [0]
 
@@ -114,15 +120,15 @@ def rank_program(g, core, T, topo):
         left[0] += engines
         return op("g", lambda: g.remote_dma_fused(xs, local_sem=T.sem["left"]), deps, "r")
 
-    d_ra = ld("y", T.TR[:, 0:24], T.rel[:, 0:384])
-    d_po = ld("s", T.PO[:, 0:3], T.pose[:, :])
-    d_rd = ld("y", T.TR[:, 24:48], T.rel[:, 192:576])
-    d_sh = ld("s", T.NB[:, 12:16], T.shown[:, :])
-    d_x = ld("s", T.X[:, :], T.x[:, :])
-    d_ct = join(ld("s", T.CT[:, 0:24], T.ct[:, 0:384]), ld("s", T.CT[:, 24:48], T.ct[:, 192:576]))
-    d_ac = ld("s", T.AC[:, 0:3], T.act[:, :])
-    d_nb = ld("s", T.NB[:, 0:12], T.nbr[:, :])
-    join(d_ra, d_rd)
+    loads = {"ra": (T.TR[:, 0:24], T.rel[:, 0:384]),
+             "rd": (T.TR[:, 24:48], T.rel[:, 192:576]),
+             "sh": (T.NB[:, 12:16], T.shown[:, :]), "po": (T.PO[:, 0:3], T.pose[:, :]), "x": (T.X[:, :], T.x[:, :]),
+             "c0": (T.CT[:, 0:24], T.ct[:, 0:384]), "c1": (T.CT[:, 24:48], T.ct[:, 192:576]),
+             "ac": (T.AC[:, 0:3], T.act[:, :]), "nb": (T.NB[:, 0:12], T.nbr[:, :])}
+    loads = {w.split(":")[0]: ld(w[-1], *loads[w.split(":")[0]]) for w in CFG["loads"].split()}
+    d_sh, d_po, d_x, d_ac, d_nb = [loads[k] for k in ("sh", "po", "x", "ac", "nb")]
+    d_rel, d_ct = join(loads["ra"], loads["rd"]), join(loads["c0"], loads["c1"])
+    join(d_ac, d_nb)
 
     def iota(out, pat, base, cm, flt=True):
         if flt:
@@ -132,30 +138,28 @@ def rank_program(g, core, T, topo):
     i_p = iota(T.IP[:, :], [[0, 2]], 0, 1, False)
     i_d = iota(T.DD[:, :], [[1, 128]], 0, -1)
     i_c = iota(T.C48[:, :], [[0, 2], [24, 48]], 0, 0)
-    i_48 = iota(T.I48[:, :], [[0, 2], [1, 24]], 0, 0)
     i_g = iota(T.GI[:, :], [[1, 8], [0, 16]], 0, 0)
     i_4 = iota(T.S4[:, :], [[24, 2], [8, 2]], -48, 0)
-    hole = 48 + 16 * r + 16
-    i_a = [iota(T.AT[:, 0:hole], [[1, hole]], 0, 0)]
-    if hole < 112:
-        i_a.append(iota(T.AT[:, hole:112], [[1, 112 - hole]], hole - 16, 0))
-    join(*i_a)
-    aeng = topo.engines(core, T.cores[near[0]])
-    send([transfer(near[0], [T.NB[:, 12 + near[0]:13 + near[0]]], T.NS[:, 0:1], aeng, "arrs")], len(aeng), [d_sh])
+    send([transfer(near[0], T.NB[:, 12 + near[0]:13 + near[0]], T.NS[:, 0:1], aeng, "arrs")], len(aeng), [d_sh])
 
     tag[0] = "cb"
     c_b = join(ts(T.B1[:, :], T.IP[:, :], 1, A.bitwise_and, deps=[i_p]),
-               ts(T.B8[:, :], T.IP[:, :], 8, A.bitwise_and, deps=[i_p]),
                ts(T.BQ[:, :], T.IP[:, :], 15, A.bitwise_and, deps=[i_p]),
-               ts(T.B7[:, :], T.IP[:, :], 7, A.bitwise_and, deps=[i_p]),
+               cp(T.PF[:, 0:1], T.IP[:, 0:1], deps=[i_p]))
+    tag[0] = "cx"
+    c_2 = join(ts(T.B7[:, :], T.IP[:, :], 7, A.bitwise_and, deps=[i_p]),
                ts(T.BG[:, :], T.IP[:, :], 4, A.arith_shift_right, deps=[i_p]))
-    c_m = join(ts(T.LO[:, :], T.B8[:, 0:1], 0, A.is_equal, deps=c_b),
-               ts(T.HI[:, :], T.B8[:, 0:1], 0, A.is_gt, deps=c_b),
+    tag[0] = "cm"
+    c_m = join(ts(T.LO[:, :], T.BQ[:, 0:1], 8, A.is_lt, deps=c_b),
+               ts(T.HI[:, :], T.BQ[:, 0:1], 8, A.is_ge, deps=c_b),
                ts(T.PQ[:, 0:1], T.B1[:, 0:1], 48, A.mult, deps=c_b),
-               ts(T.PQ[:, 1:2], T.B1[:, 0:1], -48, A.mult, 48, A.add, deps=c_b),
-               cp(T.PG[:, :], T.BG[:, 0:1], deps=c_b),
-               cp(T.QF[:, 0:1], T.BQ[:, 0:1], deps=c_b),
-               cp(T.QR[:, 0:1], T.B7[:, 0:1], deps=c_b))
+               ts(T.PQ[:, 1:2], T.B1[:, 0:1], -48, A.mult, 48, A.add, deps=c_b))
+    tag[0] = "cy"
+    c_3 = join(cp(T.PG[:, :], T.BG[:, 0:1], deps=c_2), cp(T.QF[:, 0:1], T.BQ[:, 0:1], deps=c_b), cp(T.QR[:, 0:1], T.B7[:, 0:1], deps=c_2))
+    tag[0] = "ia"
+    hole = 48 + 16 * r + 16
+    i_48 = join(*[ac(T.I48[:, 24 * k:24 * k + 24], T.DD[:, 0:24], [i_d] + c_b, bias=T.PF[:, :]) for k in range(2)])
+    i_a = join(*[ac(T.AT[:, a:b], T.DD[:, a - c:b - c], [i_d] + c_b, bias=T.PF[:, :]) for a, b, c in ((0, hole, 0), (hole, 112, 16)) if a < b])
     tag[0] = "cs"
     c_s = join(ts(T.SH[:, :], T.DD[:, :], -8, A.is_equal, T.HI[:, :], A.mult, deps=[i_d] + c_m),
                ts(T.SL[:, :], T.DD[:, :], 8, A.is_equal, T.LO[:, :], A.mult, deps=[i_d] + c_m))
@@ -166,18 +170,21 @@ def rank_program(g, core, T, topo):
     idm = ts(T.ID[:, :], T.DD[:, :], 0, A.is_equal, deps=[i_d])
     tag[0] = "on"
     zc = op("v", lambda: v.memset(T.CW[:, 48:64], 0.0))
-    c_q = ts(T.QF[:, 1:2], T.QF[:, 0:1], 8, A.add, T.HI[:, :], A.mult, deps=c_m)
-    on = ts(T.ON[:, :], T.GI[:, :], T.PG[:, :], A.is_equal, deps=[i_g] + c_m)
-    sq4 = ts(T.SQ4[:, :], T.S4[:, :], T.QF[:, 0:1], A.add, deps=[i_4] + c_m)
+    c_q = ts(T.QF[:, 1:2], T.QF[:, 0:1], 8, A.add, T.HI[:, :], A.mult, deps=c_m + c_3)
+    on = ts(T.ON[:, :], T.GI[:, :], T.PG[:, :], A.is_equal, deps=[i_g] + c_3)
+    sq4 = ts(T.SQ4[:, :], T.S4[:, :], T.QF[:, 0:1], A.add, deps=[i_4] + c_3)
+    join(zc, c_q, on, sq4)
+    join(i_c, i_g, i_4)
+    join(*(i_48 + i_a))
     tag[0] = "ch"
-    c_h = join(ac(T.SHB[:, :], T.SHW[:, :], c_f), ac(T.SLB[:, :], T.SLW[:, :], c_f), ac(T.IDB[:, :], T.ID[:, :], [idm]),
-               ac(T.LOB[:, :], T.ID[:, :], [idm] + c_m, T.LO[:, :]), ac(T.HIB[:, :], T.ID[:, :], [idm] + c_m, T.HI[:, :]))
+    c_h = join(ac(T.IDB[:, :], T.ID[:, :], [idm]),
+               ac(T.LOB[:, :], T.ID[:, :], [idm] + c_m, T.LO[:, :]), ac(T.HIB[:, :], T.ID[:, :], [idm] + c_m, T.HI[:, :]),
+               ac(T.SHB[:, :], T.SHW[:, :], c_f), ac(T.SLB[:, :], T.SLW[:, :], c_f))
     tag[0] = "at"
     i_b = ac(T.CB[:, :], T.C48[:, 0:48], [i_c])
-    i_1 = [ac(T.AT1[:, 0:48], T.AT[:, 0:48], i_a), ac(T.AT1[:, 48 + 16 * r:64 + 16 * r], T.AT[:, 0:16], i_a)]
-    for k, p in enumerate(sorted(far)):
-        i_1.append(op("s", lambda k=k, p=p: s.activation(T.AT1[:, 48 + 16 * p:64 + 16 * p], T.AT[:, 0:16], ACT.Identity, bias=96.0 + 16 * k), i_a))
-    join(*i_1)
+    i_1 = join(ac(T.AT1[:, 0:48], T.AT[:, 0:48], i_a, 8.0), ac(T.AT1[:, 48 + 16 * r:64 + 16 * r], T.AT[:, 0:16], i_a),
+               *[ac(T.AT1[:, 48 + 16 * p:64 + 16 * p], T.AT[:, 0:16], i_a, 8.0, 768.0 + 128 * k) for k, p in enumerate(sorted(far))])
+    join(i_b, *i_1)
     tag[0] = "ck"
     c_24 = join(ac(T.L24[:, :], T.LOB[:, :], c_h, 24.0), ac(T.H24[:, :], T.HIB[:, :], c_h, 24.0))
 
@@ -186,64 +193,61 @@ def rank_program(g, core, T, topo):
     tag[0] = "lh"
     lsh = join(*[ts(T.LSH[:, 4 * k:4 * k + 4], T.NB[:, 12:16], T.PQ[:, k:k + 1], A.add, deps=c_m + [d_sh]) for k in range(2)])
     tag[0] = "nn"
-    nn = tt(T.NN[:, :], T.TR[:, :].indirect(T.LP[:, 0:6]), T.C48[:, :], A.add, deps=lp + [d_ra, d_rd, i_c])
+    nn = tt(T.NN[:, :], T.TR[:, :].indirect(T.LP[:, 0:6]), T.C48[:, :], A.add, deps=lp + d_rel + [i_c])
     tag[0] = "rr"
     rr = cp(T.RR[:, :], T.NN[:, :].indirect(T.LSH[:, :]), deps=[nn] + lsh)
     tag[0] = "as"
-    as_ = ac(T.AS[:, :], T.I48[:, :].indirect(T.LP[:, :]), deps=lp + [i_48])
-    tag[0] = "o0"
-    ow = [cp(T.OWN[:, 0::3], T.NN[:, 0:48:2], deps=[nn]), cp(T.OWN[:, 2::3], T.NN[:, 49:96:2], deps=[nn])]
+    as_ = ac(T.AS[:, :], T.I48[:, :].indirect(T.LP[:, :]), deps=lp + i_48)
     tag[0] = "r0"
     la = [cp(T.LA[:, 0::3], T.RR[:, 0:64:2], deps=[rr]), cp(T.LA[:, 2::3], T.RR[:, 1:64:2], deps=[rr])]
     tag[0] = "qa"
     qa = mms([(T.PT[:, 0:32], T.SH[:, :], T.RR[:, 64:128:2]), (T.PT[:, 0:32], T.SL[:, :], T.RR[:, 65:128:2])], [rr] + c_s)
     tag[0] = "qo"
-    qo = mms([(T.PM[:, 0:24], T.SHW[:, :], T.NN[:, 48:96:2]), (T.PM[:, 0:24], T.SLW[:, :], T.NN[:, 1:48:2])], [nn] + c_f)
+    qo = join(*(mms([(T.PM[:, 1:72:3], T.SHW[:, :], T.NN[:, 48:96:2]), (T.PM[:, 1:72:3], T.SLW[:, :], T.NN[:, 1:48:2])], [nn] + c_f) +
+                mms([(T.PM[:, 0:72:3], T.ID[:, :], T.NN[:, 0:48:2])], [nn, idm]) + mms([(T.PM[:, 2:72:3], T.ID[:, :], T.NN[:, 49:96:2])], [nn, idm])))
     tag[0] = "r1"
     la.append(cp(T.LA[:, 1::3], T.PT[:, 0:32], deps=qa))
     join(*la)
-
     tag[0] = "bl"
     bl = join(*[ts(T.BL[:, 8 * k:8 * k + 8], T.ON[:, 0::16], T.SQ4[:, k:k + 1], A.mult, 48, A.add, deps=[on, sq4]) for k in range(4)])
     tag[0] = "o1"
-    ow.append(cp(T.OWN[:, 1::3], T.PM[:, 0:24], deps=qo))
-    join(*ow)
+    ow = [cp(T.OWN[:, :], T.PM[:, 0:72], deps=qo)]
     tag[0] = "rn"
-    c_r = join(ts(T.RN[:, 0:128], T.ON[:, :], T.QF[:, 0:1], A.mult, deps=[on] + c_m),
+    c_r = join(ts(T.RN[:, 0:128], T.ON[:, :], T.QF[:, 0:1], A.mult, deps=[on] + c_3),
                ts(T.RN[:, 128:256], T.ON[:, :], T.QF[:, 1:2], A.mult, deps=[on, c_q]))
-
-    def slot(p):
-        return r if r < p else r - 1
 
     for k, p in enumerate(dest):
         a, b = SLW * k, SLW * k + SLW // 2
         tag[0] = "A%d" % k
         x = join(cp(T.SA[:, a:b], T.X[:, :].indirect(T.LA[:, 24 * p:24 * p + 12]), deps=la + [d_x]),
                  ac(T.SA[:, b:a + SLW], T.X[:, :].indirect(T.LA[:, 24 * p + 12:24 * p + 24]), deps=la + [d_x]))
-        c, es = OWNW + SLW * slot(p), feng if p in far else neng
-        send([transfer(p, [T.SA[:, a:a + SLW]], T.W0[:, c:c + SLW], es, "arr0")], len(es), x)
+        c, es = OWNW + SLW * (r if r < p else r - 1), feng if p in far else neng
+        send([transfer(p, T.SA[:, a:a + SLW], T.W0[:, c:c + SLW], es, "arr0")], len(es), x)
     arr0 = [("sem", "arr0", 2 * len(feng) + len(neng))]
-    half = len(feng) // 2
-    eng1 = {far[0]: feng[:half], far[1]: feng[half:]}
     arr1 = [[("sem", "arr1_%d" % b, len(feng) + len(neng))] for b in range(3)]
 
     even0, odd0, even1, odd1 = [slice(k, k - k % 2 + 48, 2) for k in (0, 1, 48, 49)]
-    picks = [((T.LOB, even0), (T.SLB, odd0)), ((T.LOB, even1), (T.HIB, odd0)), ((T.SHB, even1), (T.HIB, odd1))]
     bv = CFG["bv"]
 
     def rows(out, oh, deps):
         return join(*sum([mms([(out[:, 48 * h:48 * h + 48], T.BD[:, 256 * k + 128 * h:256 * k + 128 * h + 128], oh[:, 48 * k:48 * k + 48])
                                for k in range(2)], deps) for h in range(2)], []))
 
+    def parts(uu, one, eight):
+        return join(ts(uu[:, 96:192], T.UD[:, 0:96], 8, A.is_ge, eight, A.mult, deps=["ra"]),
+                    ts(uu[:, 192:288], T.UD[:, 0:96], 16, A.is_ge, eight, A.mult, deps=["ra"]))
 
-    def natural():
-        parts = [T.UU[:, 96 * k:96 * k + 96] for k in range(3)]
-        P, d = T.PM, ["uu"] + ow + c_h + [i_b]
+    def natural(P, uu, node, d):
+        xs = [uu[:, 96 * k:96 * k + 96] for k in range(3)]
+        c0, c1, c2 = [P[:, k:72:3] for k in range(3)]
         return join(*(
-            mms([(P[:, 0:24], T.IDB[:, :], T.CB[:, even0])] + [(P[:, 0:24], T.IDB[:, :], x[:, even0]) for x in parts], d) +
-            mms([(P[:, 24:48], T.LOB[:, :], T.CB[:, even0]), (P[:, 24:48], T.HIB[:, :], T.CB[:, odd0])] +
-                [(P[:, 24:48], T.SHB[:, :], x[:, even1]) for x in parts] + [(P[:, 24:48], T.SLB[:, :], x[:, odd0]) for x in parts], d) +
-            mms([(P[:, 48:72], T.IDB[:, :], T.CB[:, odd0])] + [(P[:, 48:72], T.IDB[:, :], x[:, odd1]) for x in parts], d)))
+            mms([(c0, T.IDB[:, :], node[:, even0])] + [(c0, T.IDB[:, :], x[:, even0]) for x in xs], d) +
+            mms([(c1, T.LOB[:, :], node[:, even0]), (c1, T.HIB[:, :], node[:, odd0])] +
+                [(c1, T.SHB[:, :], x[:, even1]) for x in xs] + [(c1, T.SLB[:, :], x[:, odd0]) for x in xs], d) +
+            mms([(c2, T.IDB[:, :], node[:, odd0])] + [(c2, T.IDB[:, :], x[:, odd1]) for x in xs], d)))
+
+    def halves(out, x):
+        return [(out, T.LOB[:, :], x[:, 0::2]), (out, T.HIB[:, :], x[:, 1::2])]
 
     step = {
         "cw": lambda: join(cp(T.CW[:, 0:24], T.CT[:, 0:24], deps=d_ct),
@@ -260,25 +264,29 @@ def rank_program(g, core, T, topo):
         "ok": lambda: [tt(T.OK[:, :], T.CA[:, :], T.PS[:, 0:96], A.is_equal, deps=["qs", "ca"])],
         "qk": lambda: rows(T.PK, T.OK, ["ok", "bs", "bw"]),
         "rw": lambda: [cp(T.RW[:, :], T.PK[:, 0:96], deps=["qk"])],
-        "qe": lambda: join(*sum([mms([(T.PJ[:, 8 * k:8 * k + 8], m[:, :], T.ARM[:, 192 + 16 * p + h:208 + 16 * p:2])
-                                      for h, m in enumerate((T.LOB, T.HIB))], ["ar"] + c_h) for k, p in enumerate(sorted(far))], [])),
-        "le": lambda: [ts(T.LF[:, 96:112], T.PJ[:, 0:16], 8, A.mult, T.QR[:, :], A.add, deps=["qe"] + c_m)],
+        "qe": lambda: join(*sum([mms(halves(T.PJ[:, 8 * k:8 * k + 8], T.ARM[:, 192 + 16 * p:208 + 16 * p]), ["ar"] + c_h)
+                                 for k, p in enumerate(far)], [])),
+        "le": lambda: [ts(T.LE[:, :], T.PJ[:, 0:16], 8, A.mult, T.QR[:, :], A.add, deps=["qe"] + c_3)],
         "nu": lambda: [cp(T.NSU[:, 0:1], T.NS[:, 0:1], deps=[("sem", "arrs", len(aeng))])],
-        "nt": lambda: [ts(T.AT1[:, 48 + 16 * near[0]:64 + 16 * near[0]], T.AT[:, 0:48].indirect(T.NSU[:, 0:1]), 48, A.add, deps=i_a + ["nu"])],
+        "nt": lambda: [ts(T.AT1[:, 48 + 16 * near[0]:64 + 16 * near[0]], T.AT[:, 0:48].indirect(T.NSU[:, 0:1]), 48, A.add, 8, A.mult,
+                          deps=i_a + ["nu"])],
         "an": lambda: [ac(T.AR1[:, :], T.AT1[:, :].indirect(T.NBU[:, 0:12]), deps=i_1 + ["nb", "nt"])],
-        "qj": lambda: mms([(T.PJ[:, 0:96], T.LOB[:, :], T.AR1[:, 0::2]), (T.PJ[:, 0:96], T.HIB[:, :], T.AR1[:, 1::2])], ["an", "le"] + c_h),
-        "lf": lambda: [ts(T.LF[:, 0:96], T.PJ[:, 0:96], 8, A.mult, T.QR[:, :], A.add, deps=["qj"] + c_m)],
+        "qj": lambda: mms(halves(T.PJ[:, 0:96], T.AR1[:, :]), ["an", "le"] + c_h),
+        "lf": lambda: [ts(T.LF[:, :], T.PJ[:, 0:96], T.QR[:, :], A.add, deps=["qj"] + c_3)],
         "xs": lambda: [ac(T.W0[:, 24 * bv:OWNW], T.X[:, :].indirect(T.OWN[:, bv * 3 // 2:72]), deps=ow + [d_x])],
         "xv": lambda: [cp(T.W0[:, 0:24 * bv], T.X[:, :].indirect(T.OWN[:, 0:bv * 3 // 2]), deps=ow + [d_x])] if bv else [],
-        "ms": lambda: [ac(T.MS[:, :], T.I48[:, :].indirect(T.LM[:, :]), deps=["lm", i_48])],
+        "ms": lambda: [ac(T.MS[:, :], T.I48[:, :].indirect(T.LM[:, :]), deps=["lm"] + i_48)],
         "oa": lambda: [tt(T.OA[:, :], T.TR[:, :].indirect(T.LP[:, :]), T.MS[:, :], A.is_equal, deps=["ms"])],
         "qy": lambda: rows(T.PT, T.OA, ["oa", "bs", "bw"] + la),
-        "uu": lambda: join(ts(T.UU[:, 0:96], T.PT[:, 0:96], 3, A.mult, deps=["qy"]),
-                           ts(T.UU[:, 96:192], T.PT[:, 0:96], 8, A.is_ge, -23, A.mult, deps=["qy"]),
-                           ts(T.UU[:, 192:288], T.PT[:, 0:96], 16, A.is_ge, -23, A.mult, deps=["qy"])),
-        "qz": natural,
-        "ly": lambda: join(*[cp(T.LY[:, k::3], T.PM[:, 24 * k:24 * k + 24], deps=["qz"]) for k in range(3)]),
+        "ra": lambda: join(ac(T.UD[:, 0:96], T.PT[:, 0:96], ["qy"]), ac(T.UU[:, 0:96], T.PT[:, 0:96], ["qy"], 3.0)),
+        "uu": lambda: parts(T.UU, 3, -23),
+        "qz": lambda: natural(T.PM, T.UU, T.CB, ["uu", i_b] + ow + c_h),
+        "ly": lambda: [cp(T.LY[:, :], T.PM[:, 0:72], deps=["qz"])],
+        "ud": lambda: parts(T.UD, 1, BLK - 8),
+        "qd": lambda: natural(T.PK, T.UD, T.AR1[:, 144:192], ["ud", "an", "rw"] + c_h),
+        "ld": lambda: [cp(T.LD[:, :], T.PK[:, 0:72], deps=["qd"])],
     }
+    picks = [((T.LOB, even0), (T.SLB, odd0)), ((T.LOB, even1), (T.HIB, odd0)), ((T.SHB, even1), (T.HIB, odd1))]
     for b in range(3):
         step["j%d" % b] = lambda b=b: mms([(T["PL%d" % b][:, 0:96], m[:, :], T.ARM[:, h:192:2]) for h, m in enumerate((T.L24, T.H24))],
                                           ["ar"] + c_24, last=False)
@@ -286,97 +294,115 @@ def rank_program(g, core, T, topo):
                                           ["rw"] + c_h, first=False)
         step["l%d" % b] = lambda b=b: [cp(T.LC[:, 96 * b:96 * b + 96], T["PL%d" % b][:, 0:96], deps=["q%d" % b])]
 
-    banks = [[T.PS, ["ok"]], [T.PK, ["rw"]], [T.PL0, ["l0"]], [T.PL1, ["l1"]], [T.PL2, ["l2"]], [T.PJ, ["lf"]]]
+    banks = [[T.PS, ["ok"]], [T.PL0, ["l0"]], [T.PL1, ["l1"]], [T.PL2, ["l2"]], [T.PJ, ["lf"]], [T.PK, ["ld" if CFG["four"] < 48 else "rw"]]]
     turn = [0]
     own0 = ["xs", "xv"]
     P = {}
     at = 0
     for k, (rd, b, i0, n, kv) in CFG["P"].items():
-        w = 8 * n
-        j = {"rd": rd, "b": b, "i0": i0, "n": n, "kv": kv, "w": w}
+        j = {"rd": rd, "b": b, "i0": i0, "n": n, "kv": kv, "w": 8 * n, "at": at, "last": 2 if rd == 0 or i0 < CFG["four"] else 1}
         if rd == 0:
-            win, lst, c0 = T.W0[:, :], T.LC, 96 * b
+            win, lst, c0 = T.W0[:, :], T.LC, 96 * b + i0 // 2
             j["deps"], j["out"] = ["l%d" % b] + own0 + arr0, T.W1[:, BLK * b + 8 * i0:BLK * b + 8 * (i0 + n)]
         else:
-            win, lst, c0 = T.W1[:, BLK * b:BLK * b + BLK], T.LF, 0
+            win, lst, c0 = T.W1[:, BLK * b:BLK * b + BLK], T.LF, i0 // 2
             j["deps"], j["out"] = ["lf", "W%d" % b] + arr1[b], T.MP[:, 24 * i0 + b:24 * (i0 + n):3]
-        j.update({"win": win, "lst": lst, "c0": c0 + i0 // 2, "at": at})
-        j["src"] = [win.indirect(lst[:, j["c0"] + 24 * m:j["c0"] + 24 * m + n // 2]) for m in range(4)]
-        j["G"] = T.G0[:, at:at + w]
-        j["H"] = [T["H%d" % m][:, at:at + w] for m in range(2)]
-        at += w
+        j["src"] = [win.indirect(lst[:, c0 + 24 * m:c0 + 24 * m + n // 2]) for m in range(4)]
+        j["G"] = [T["G%d" % m][:, at:at + 8 * n] for m in range(3)]
+        j["H"] = [T["H%d" % m][:, at:at + 8 * n] for m in range(2)]
+        at += 8 * n
         P[k] = j
 
-    def scalar_step(ks, m):
-        j, w = P[ks[0]], sum(P[k]["w"] for k in ks)
-        c = j["c0"] + 24 * (3 - m)
-        x = ac(T["G%d" % m][:, j["at"]:j["at"] + w], j["win"].indirect(j["lst"][:, c:c + w // 16]), j["deps"])
-        for k in ks:
-            named[k + ("g0" if m == 0 else "s%d" % m)] = [x]
+    def scalar_step(k, m):
+        j = P[k]
+        named[k + ("g0" if m == 0 else "s%d" % m)] = [ac(j["G"][m], j["src"][j["last"] + 1 - m], j["deps"])]
 
-    def tensor_step(ks, m):
-        j, w = P[ks[0]], sum(P[k]["w"] for k in ks)
+    def tensor_step(k, m):
+        j = P[k]
         bank = banks[turn[0] % len(banks)]
         turn[0] += 1
-        x = mms([(bank[0][:, 0:w], T.ID[:, :], T["G%d" % m][:, j["at"]:j["at"] + w])], [k + "s%d" % m for k in ks] + [idm] + bank[1])
-        for k in ks:
-            c = P[k]["at"] - j["at"]
-            P[k]["P%d" % m], named[k + "g%d" % m] = bank[0][:, c:c + P[k]["w"]], x
-        bank[1] = [k + "v%d" % (P[k]["kv"] + m - 1) for k in ks]
+        j["P%d" % m] = bank[0][:, 0:j["w"]]
+        named[k + "g%d" % m] = mms([(j["P%d" % m], T.ID[:, :], j["G"][m])], [k + "s%d" % m, idm] + bank[1])
+        bank[1] = [k + "v%d" % (j["kv"] + m - 1)]
 
     def vector_step(k, m):
         j = P[k]
         kv = j["kv"]
-        out = j["out"] if m == 2 else j["H"][m]
-        prev = (j["G"], k + "g0") if m == 0 else (j["H"][m - 1], k + "v%d" % (m - 1))
+        out = j["out"] if m == j["last"] else j["H"][m]
+        prev = (j["G"][0], k + "g0") if m == 0 else (j["H"][m - 1], k + "v%d" % (m - 1))
         if m < kv:
             x = tt(out, j["src"][m], prev[0], A.max, j["deps"] + [prev[1]])
         else:
             u = m - kv + 1
             x = tt(out, prev[0], j["P%d" % u], A.max, [prev[1], k + "g%d" % u])
         named[k + "v%d" % m] = [x]
-        if m == 2:
-            named.setdefault(("W%d" if j["rd"] == 0 else "M%d") % j["b"], []).append(x)
+        if m == j["last"]:
+            named.setdefault("WM"[j["rd"]] + str(j["b"]), []).append(x)
             named[k + "done"] = [x]
 
     def shown(b, q, lo, hi):
-        f = ac if q == "s" else cp
-        named.setdefault("E%d" % b, []).append(
-            f(T.EX[:, 256 * b + 16 * lo:256 * b + 16 * hi], T.W1[:, BLK * b:BLK * b + 384].indirect(T.LF[:, 96 + lo:96 + hi]), ["le", "W%d" % b]))
+        named.setdefault("E%d" % b, []).append((ac if q == "s" else cp)(
+            T.EX[:, 256 * b + 8 * lo:256 * b + 8 * hi], T.W1[:, BLK * b:BLK * b + 384].indirect(T.LE[:, lo // 2:hi // 2]), ["le", "W%d" % b]))
 
-    finals = []
+    def shown_parts(b, q):
+        ks = [k for k in P if P[k]["rd"] == 0 and P[k]["b"] == b]
+        c = P[ks[0]]["at"]
+        if q == "s":
+            named["EG%d" % b] = [ac(T.EG[:, 256 * b:256 * b + 256], T.G1[:, c:c + 384].indirect(T.LE[:, :]), ["le"] + [k + "s1" for k in ks])]
+        else:
+            named["E%d" % b] = [tt(T.EX[:, 256 * b:256 * b + 256], T.H1[:, c:c + 384].indirect(T.LE[:, :]), T.EG[:, 256 * b:256 * b + 256],
+                                   A.max, ["le", "EG%d" % b] + [k + "v1" for k in ks])]
+
+    finals, fourth = [], []
+
+    def framed(b):
+        return ["ly"] + [x + "done" for x in P if P[x]["rd"] == 1 and P[x]["i0"] < b]
 
     def final(q, a, b):
-        f = ac if q == "s" else cp
-        finals.append((a, b, f(T.YB[:, 24 * a:24 * b], T.MP[:, 0:24 * b].indirect(T.LY[:, a * 3 // 2:b * 3 // 2]),
-                               ["ly"] + [x + "done" for x in P if P[x]["rd"] == 1 and P[x]["i0"] < b])))
+        finals.append((a, b, (ac if q == "s" else cp)(T.YB[:, 24 * a:24 * b], T.MP[:, 0:24 * b].indirect(T.LY[:, a * 3 // 2:b * 3 // 2]), framed(b))))
+
+    def direct(a, b):
+        fourth.append((a, b, ac(T.DB[:, 24 * a:24 * b], T.W1[:, :].indirect(T.LD[:, a * 3 // 2:b * 3 // 2]),
+                                ["ld", "W0", "W1", "W2"] + sum(arr1, []))))
+
+    def joined(a, b):
+        finals.append((a, b, tt(T.YB[:, 24 * a:24 * b], T.MP[:, 0:24 * b].indirect(T.LY[:, a * 3 // 2:b * 3 // 2]), T.DB[:, 24 * a:24 * b],
+                                A.max, framed(b) + [d for lo, hi, d in fourth if lo < b and a < hi])))
 
     early = set(o["tag"] for o in ops)
     for q in "tsv":
         for w in CFG[q.upper()].split():
             tag[0] = w
-            w, lo, hi = (w.split(":") + [0, 48])[:3]
+            w, lo, hi = (w.split(":") + [0, 32])[:3]
             if w in early:
                 continue
             if w[0] == "E":
-                shown(int(w[1]), q, int(lo), min(int(hi), 16))
+                shown(int(w[1]), q, int(lo), int(hi))
+            elif w[0] == "F":
+                shown_parts(int(w[1]), q)
             elif w[0] == "Y":
                 final(q, int(lo), int(hi))
+            elif w[0] in "DZ":
+                (direct if w[0] == "D" else joined)(int(lo), int(hi))
             elif w in step:
                 named[w] = step[w]()
-            elif q == "t":
-                tensor_step(w[:-1], int(w[-1]))
-            elif q == "s":
-                scalar_step(w[:-1], int(w[-1]))
             else:
-                vector_step(w[0], int(w[1]))
+                {"t": tensor_step, "s": scalar_step, "v": vector_step}[q](w[0], int(w[1]))
 
-    for b in range(3):
-        c = BLK * b
-        send([transfer(near[0], [T.W1[:, c:c + 384]], T.W1[:, c + 384:c + 768], neng, "arr1_%d" % b)], len(neng), ["W%d" % b])
-        c += 768 + 128 * sorted([r] + near).index(r)
-        send([transfer(p, [T.EX[:, 256 * b + 128 * k:256 * b + 128 * k + 128]], T.W1[:, c:c + 128], eng1[p], "arr1_%d" % b)
-              for k, p in enumerate(sorted(far))], len(feng), ["E%d" % b])
+    for a, b in (("bs", "bw"), ("xs", "xv")):
+        join(*(named[a] + named[b]))
+    join(*(lp + lsh))
+    join(idm, *c_f)
+    half = len(feng) // 2
+    for w in CFG["G"].split():
+        b = int(w[1])
+        c, arr = BLK * b, "arr1_%d" % b
+        if w[0] == "n":
+            send([transfer(near[0], T.W1[:, c:c + 384], T.W1[:, c + 384:c + 768], neng, arr)], len(neng), ["W%d" % b])
+        else:
+            c += 768 + 128 * sorted([r] + near).index(r)
+            send([transfer(p, T.EX[:, 256 * b + 128 * k:256 * b + 128 * k + 128], T.W1[:, c:c + 128], feng[half * k:half * k + half], arr)
+                  for k, p in enumerate(far)], len(feng), ["E%d" % b])
     stores = []
     for a, b in zip(CFG["stores"], CFG["stores"][1:]):
         stores.append(ld("y", T.y[:, 24 * a:24 * b], T.YB[:, 24 * a:24 * b], [x for lo, hi, x in finals if lo < b and a < hi]))
@@ -385,6 +411,8 @@ def rank_program(g, core, T, topo):
 
     for o in ops:
         o["deps"] = sum([named[d] if isinstance(d, str) else [d] for d in o["deps"]], [])
+    if "hook" in CFG:
+        CFG["hook"](ops)
     used, total = set(), {}
     for o in ops:
         used.update(ops[d]["grp"] for d in o["deps"] if not isinstance(d, tuple))
@@ -392,18 +420,7 @@ def rank_program(g, core, T, topo):
         total[o["grp"]] = total.get(o["grp"], 0) + (16 if o["kind"] == "d" else 1)
     order = {q: CFG.get(q.upper(), "").split() for q in queues}
     seq = sorted(ops, key=lambda o: order[o["q"]].index(o["tag"]) if o["q"] in "vst" and o["kind"] == "c" else -1)
-    seen, before = {q: set() for q in queues}, {}
-    for o in seq:
-        seen[o["q"]].update(ops[d]["grp"] for d in o["deps"] if not isinstance(d, tuple) and ops[d]["kind"] == "c")
-        before[o["grp"]] = before.get(o["grp"], seen[o["q"]]) & seen[o["q"]]
-    names, taken, spare = {}, set(), len(used) - NX
-    for k in sorted(used):
-        free = sorted(a for a in before[k] if a in names and a not in taken)
-        if spare > 0 and free and ops[k]["kind"] == "c":
-            taken.add(free[0])
-            names[k], total[k], spare = names[free[0]], total[k] + total[free[0]], spare - 1
-        else:
-            names[k] = "x%d" % len(set(names.values()))
+    names = {k: "x%d" % n for n, k in enumerate(sorted(used))}
     done = {q: {} for q in queues}
 
     def wait(q, name, val):

from concourse.bass import DstId, RemoteDMATransfer
from concourse.mybir import AluOpType, ActivationFunctionType

NX = 144
SCRATCH = {
    "X": ("sbuf", [128, 1152], "float32"), "TR": ("sbuf", [128, 48], "int32"), "PO": ("sbuf", [128, 4], "int32"),
    "NB": ("sbuf", [128, 16], "int32"), "AC": ("sbuf", [128, 4], "int32"), "CT": ("sbuf", [128, 48], "int32"),
    "NS": ("sbuf", [128, 4], "int32"),
    "IP": ("sbuf", [128, 2], "int32"), "DD": ("sbuf", [128, 128], "float32"), "GI": ("sbuf", [128, 128], "float32"),
    "C48": ("sbuf", [128, 96], "float32"), "CB": ("sbuf", [128, 48], "bfloat16"), "S4": ("sbuf", [128, 4], "float32"),
    "SQ4": ("sbuf", [128, 4], "float32"), "AT": ("sbuf", [128, 112], "float32"), "I48": ("sbuf", [128, 48], "float32"),
    "AT1": ("sbuf", [128, 112], "float32"),
    "B1": ("sbuf", [128, 2], "int32"), "BQ": ("sbuf", [128, 2], "int32"),
    "B7": ("sbuf", [128, 2], "int32"), "QR": ("sbuf", [128, 1], "float32"), "PF": ("sbuf", [128, 1], "float32"),
    "BG": ("sbuf", [128, 2], "int32"), "PG": ("sbuf", [128, 1], "float32"), "QF": ("sbuf", [128, 2], "float32"),
    "LO": ("sbuf", [128, 1], "float32"), "HI": ("sbuf", [128, 1], "float32"), "PQ": ("sbuf", [128, 2], "float32"),
    "SH": ("sbuf", [128, 128], "float16"), "SL": ("sbuf", [128, 128], "float16"), "ON": ("sbuf", [128, 128], "bfloat16"),
    "SHW": ("sbuf", [128, 128], "float32"), "SLW": ("sbuf", [128, 128], "float32"), "ID": ("sbuf", [128, 128], "float32"),
    "SHB": ("sbuf", [128, 128], "bfloat16"), "SLB": ("sbuf", [128, 128], "bfloat16"), "IDB": ("sbuf", [128, 128], "bfloat16"),
    "LOB": ("sbuf", [128, 128], "bfloat16"), "HIB": ("sbuf", [128, 128], "bfloat16"),
    "L24": ("sbuf", [128, 128], "bfloat16"), "H24": ("sbuf", [128, 128], "bfloat16"),
    "RN": ("sbuf", [128, 256], "bfloat16"), "BL": ("sbuf", [128, 32], "uint16"),
    "LP": ("sbuf", [128, 6], "uint16"), "LM": ("sbuf", [128, 6], "uint16"),
    "NN": ("sbuf", [128, 96], "float32"), "LSH": ("sbuf", [128, 8], "uint16"),
    "RR": ("sbuf", [128, 128], "float16"), "LA": ("sbuf", [128, 96], "uint16"), "OWN": ("sbuf", [128, 72], "uint16"),
    "NBU": ("sbuf", [128, 16], "uint16"), "CW": ("sbuf", [128, 64], "float32"), "BD": ("sbuf", [128, 512], "bfloat16"),
    "AS": ("sbuf", [128, 96], "float32"), "MS": ("sbuf", [128, 96], "float32"), "CA": ("sbuf", [128, 96], "float32"),
    "OA": ("sbuf", [128, 96], "bfloat16"), "OS": ("sbuf", [128, 96], "bfloat16"), "OK": ("sbuf", [128, 96], "bfloat16"),
    "ARM": ("sbuf", [128, 256], "bfloat16"), "RW": ("sbuf", [128, 96], "bfloat16"),
    "UU": ("sbuf", [128, 288], "bfloat16"), "UD": ("sbuf", [128, 288], "bfloat16"),
    "AR1": ("sbuf", [128, 192], "bfloat16"), "NSU": ("sbuf", [128, 2], "uint16"),
    "LC": ("sbuf", [128, 288], "uint16"), "LF": ("sbuf", [128, 96], "uint16"), "LE": ("sbuf", [128, 16], "uint16"),
    "LY": ("sbuf", [128, 72], "uint16"), "LD": ("sbuf", [128, 72], "uint16"),
    "W0": ("sbuf", [128, 2304], "float32"), "W1": ("sbuf", [128, 3072], "float32"),
    "SA": ("sbuf", [128, 1152], "float32"), "EX": ("sbuf", [128, 768], "float32"), "EG": ("sbuf", [128, 768], "float32"),
    "MP": ("sbuf", [128, 1152], "float32"), "YB": ("sbuf", [128, 1152], "float32"), "DB": ("sbuf", [128, 1152], "float32"),
    "G0": ("sbuf", [128, 2304], "float32"), "G1": ("sbuf", [128, 2304], "float32"), "G2": ("sbuf", [128, 2304], "float32"),
    "H0": ("sbuf", [128, 2304], "float32"), "H1": ("sbuf", [128, 2304], "float32"),
    "PT": ("psum", [128, 512], "float32"), "PM": ("psum", [128, 512], "float32"), "PS": ("psum", [128, 512], "float32"),
    "PK": ("psum", [128, 512], "float32"), "PJ": ("psum", [128, 512], "float32"),
    "PL0": ("psum", [128, 512], "float32"), "PL1": ("psum", [128, 512], "float32"), "PL2": ("psum", [128, 512], "float32"),
}
SEMAPHORES = ["left", "arrs", "arr0"] + ["arr1_%d" % b for b in range(3)] + ["x%d" % k for k in range(NX)]
OWNW, SLW, BLK = 48 * 24, 16 * 24, 128 * 8
CFG = {
    "bv": 12, "four": 32, "G": "n0 f0 n1 f1 f2 n2", "e8": 1, "loads": "ra:y sh:s po:s rd:y x:s c0:s c1:s ac:s nb:s",
    "P": {"a": (0, 0, 0, 24, 2), "b": (0, 0, 24, 24, 2), "c": (0, 1, 0, 48, 2), "d": (0, 2, 0, 48, 2),
          "e": (1, 0, 0, 32, 2), "f": (1, 0, 32, 16, 2), "g": (1, 1, 0, 32, 2), "h": (1, 1, 32, 16, 2),
          "i": (1, 2, 0, 16, 2), "k": (1, 2, 16, 16, 2), "m": (1, 2, 32, 16, 2)},
    "T": "qa qo qs qk j1 j0 qe qy q0 j2 q1 q2 qj a1 b1 c1 qz qd d1 e1 g1 i1 k1",
    "S": "ia as at ch A0 A1 A2 ca ms ck bs ar xs an ra a0 b0 a1 b1 c0 c1 E0 d0 d1 E1 F2 e0 f0 e1 g0 h0 g1 i0 i1 k0 m0 k1 "
         "D:32:48 Y:0:16 Y:16:32",
    "V": "cb cx cm cy cs lh lp id nn cf rr on r0 r1 A0 A1 lm cw A2 rn bl oa nb os nu o1 bw ok nt rw xv l0 l2 l1 le "
         "a0 b0 a1 b1 uu a2 b2 c0 ud c1 lf c2 d0 ly d1 ld F2 d2 e0 f0 e1 f1 e2 g0 h0 g1 i0 g2 i1 k0 i2 k1 m0 k2 h1 m1 Z:32:48",
    "stores": (0, 16, 32, 48),
}


def rank_program(g, core, T, topo):
    r = T.rank_of(core)
    if r is None:
        return
    A, ACT = AluOpType, ActivationFunctionType
    ops, named, tag = [], {}, [None]

    def op(q, f, deps=(), kind="c"):
        ops.append({"q": q, "f": f, "deps": list(deps), "kind": kind, "grp": len(ops), "tag": tag[0]})
        return len(ops) - 1

    def join(*ks):
        for k in ks:
            ops[k]["grp"] = ks[0]
        return list(ks)

    v, s, t = g.vector, g.scalar, g.tensor
    queues = {"v": v, "s": s, "t": t, "g": g, "y": g.sync}

    def ts(out, in0, s1, op0, s2=None, op1=None, deps=()):
        if op1 is None:
            return op("v", lambda: v.tensor_scalar(out, in0, s1, None, op0), deps)
        return op("v", lambda: v.tensor_scalar(out, in0, s1, s2, op0, op1), deps)

    def tt(out, a, b, o, deps=()):
        return op("v", lambda: v.tensor_tensor(out, a, b, o), deps)

    def cp(out, a, deps=()):
        return op("v", lambda: v.tensor_copy(out, a), deps)

    def ac(out, a, deps=(), scale=1.0, bias=None):
        if bias is None:
            return op("s", lambda: s.activation(out, a, ACT.Copy, scale=scale), deps)
        return op("s", lambda: s.activation(out, a, ACT.Identity, bias=bias, scale=scale), deps)

    def mms(terms, deps, first=True, last=True):
        def mm(out, lhs, rhs, k):
            return op("t", lambda: t.matmul(out, lhs, rhs, first and k == 0, last and k == len(terms) - 1), deps)
        return join(*[mm(o, l, x, k) for k, (o, l, x) in enumerate(terms)])

    def ld(q, out, in_, deps=()):
        return op(q, lambda: queues[q].dma_start(out, in_), deps, "d")

    others = [p for p in range(len(T.cores)) if p != r]
    near = [p for p in others if T.cores[p] in topo.cores_of(core)]
    far = [p for p in others if p not in near]
    far.sort(key=lambda p: topo.die(T.cores[p]) != topo.die(core))
    dest = far[:1] + near + far[1:] if CFG.get("e8") == 1 else far + near
    feng = topo.engines(core, T.cores[far[0]])
    aeng = topo.engines(core, T.cores[near[0]])
    neng = [e for e in aeng if e not in feng]
    aeng = feng if CFG.get("e8") else aeng

    def transfer(p, src, dst, es, arr):
        rid, pid = topo.addr(T.cores[p], core)
        return RemoteDMATransfer(srcs=[src], dsts=[dst], dst_ids=[DstId(rid=rid, pnc=pid)], dma_engine_mask=sum(1 << e for e in es),
                                 remote_sem=T.sem[arr])

    left = [0]

    def send(xs, engines, deps):
        left[0] += engines
        return op("g", lambda: g.remote_dma_fused(xs, local_sem=T.sem["left"]), deps, "r")

    loads = {"ra": (T.TR[:, 0:24], T.rel[:, 0:384]),
             "rd": (T.TR[:, 24:48], T.rel[:, 192:576]),
             "sh": (T.NB[:, 12:16], T.shown[:, :]), "po": (T.PO[:, 0:3], T.pose[:, :]), "x": (T.X[:, :], T.x[:, :]),
             "c0": (T.CT[:, 0:24], T.ct[:, 0:384]), "c1": (T.CT[:, 24:48], T.ct[:, 192:576]),
             "ac": (T.AC[:, 0:3], T.act[:, :]), "nb": (T.NB[:, 0:12], T.nbr[:, :])}
    loads = {w.split(":")[0]: ld(w[-1], *loads[w.split(":")[0]]) for w in CFG["loads"].split()}
    d_sh, d_po, d_x, d_ac, d_nb = [loads[k] for k in ("sh", "po", "x", "ac", "nb")]
    d_rel, d_ct = join(loads["ra"], loads["rd"]), join(loads["c0"], loads["c1"])
    join(d_ac, d_nb)

    def iota(out, pat, base, cm, flt=True):
        if flt:
            return op("g", lambda: g.iota(out, pat, base, cm, allow_small_or_imprecise_dtypes=True))
        return op("g", lambda: g.iota(out, pat, base, cm))

    i_p = iota(T.IP[:, :], [[0, 2]], 0, 1, False)
    i_d = iota(T.DD[:, :], [[1, 128]], 0, -1)
    i_c = iota(T.C48[:, :], [[0, 2], [24, 48]], 0, 0)
    i_g = iota(T.GI[:, :], [[1, 8], [0, 16]], 0, 0)
    i_4 = iota(T.S4[:, :], [[24, 2], [8, 2]], -48, 0)
    send([transfer(near[0], T.NB[:, 12 + near[0]:13 + near[0]], T.NS[:, 0:1], aeng, "arrs")], len(aeng), [d_sh])

    tag[0] = "cb"
    c_b = join(ts(T.B1[:, :], T.IP[:, :], 1, A.bitwise_and, deps=[i_p]),
               ts(T.BQ[:, :], T.IP[:, :], 15, A.bitwise_and, deps=[i_p]),
               cp(T.PF[:, 0:1], T.IP[:, 0:1], deps=[i_p]))
    tag[0] = "cx"
    c_2 = join(ts(T.B7[:, :], T.IP[:, :], 7, A.bitwise_and, deps=[i_p]),
               ts(T.BG[:, :], T.IP[:, :], 4, A.arith_shift_right, deps=[i_p]))
    tag[0] = "cm"
    c_m = join(ts(T.LO[:, :], T.BQ[:, 0:1], 8, A.is_lt, deps=c_b),
               ts(T.HI[:, :], T.BQ[:, 0:1], 8, A.is_ge, deps=c_b),
               ts(T.PQ[:, 0:1], T.B1[:, 0:1], 48, A.mult, deps=c_b),
               ts(T.PQ[:, 1:2], T.B1[:, 0:1], -48, A.mult, 48, A.add, deps=c_b))
    tag[0] = "cy"
    c_3 = join(cp(T.PG[:, :], T.BG[:, 0:1], deps=c_2), cp(T.QF[:, 0:1], T.BQ[:, 0:1], deps=c_b), cp(T.QR[:, 0:1], T.B7[:, 0:1], deps=c_2))
    tag[0] = "ia"
    hole = 48 + 16 * r + 16
    i_48 = join(*[ac(T.I48[:, 24 * k:24 * k + 24], T.DD[:, 0:24], [i_d] + c_b, bias=T.PF[:, :]) for k in range(2)])
    i_a = join(*[ac(T.AT[:, a:b], T.DD[:, a - c:b - c], [i_d] + c_b, bias=T.PF[:, :]) for a, b, c in ((0, hole, 0), (hole, 112, 16)) if a < b])
    tag[0] = "cs"
    c_s = join(ts(T.SH[:, :], T.DD[:, :], -8, A.is_equal, T.HI[:, :], A.mult, deps=[i_d] + c_m),
               ts(T.SL[:, :], T.DD[:, :], 8, A.is_equal, T.LO[:, :], A.mult, deps=[i_d] + c_m))
    tag[0] = "cf"
    c_f = join(ts(T.SHW[:, :], T.DD[:, :], -8, A.is_equal, T.HI[:, :], A.mult, deps=[i_d] + c_m),
               ts(T.SLW[:, :], T.DD[:, :], 8, A.is_equal, T.LO[:, :], A.mult, deps=[i_d] + c_m))
    tag[0] = "id"
    idm = ts(T.ID[:, :], T.DD[:, :], 0, A.is_equal, deps=[i_d])
    tag[0] = "on"
    zc = op("v", lambda: v.memset(T.CW[:, 48:64], 0.0))
    c_q = ts(T.QF[:, 1:2], T.QF[:, 0:1], 8, A.add, T.HI[:, :], A.mult, deps=c_m + c_3)
    on = ts(T.ON[:, :], T.GI[:, :], T.PG[:, :], A.is_equal, deps=[i_g] + c_3)
    sq4 = ts(T.SQ4[:, :], T.S4[:, :], T.QF[:, 0:1], A.add, deps=[i_4] + c_3)
    join(zc, c_q, on, sq4)
    join(i_c, i_g, i_4)
    join(*(i_48 + i_a))
    tag[0] = "ch"
    c_h = join(ac(T.IDB[:, :], T.ID[:, :], [idm]),
               ac(T.LOB[:, :], T.ID[:, :], [idm] + c_m, T.LO[:, :]), ac(T.HIB[:, :], T.ID[:, :], [idm] + c_m, T.HI[:, :]),
               ac(T.SHB[:, :], T.SHW[:, :], c_f), ac(T.SLB[:, :], T.SLW[:, :], c_f))
    tag[0] = "at"
    i_b = ac(T.CB[:, :], T.C48[:, 0:48], [i_c])
    i_1 = join(ac(T.AT1[:, 0:48], T.AT[:, 0:48], i_a, 8.0), ac(T.AT1[:, 48 + 16 * r:64 + 16 * r], T.AT[:, 0:16], i_a),
               *[ac(T.AT1[:, 48 + 16 * p:64 + 16 * p], T.AT[:, 0:16], i_a, 8.0, 768.0 + 128 * k) for k, p in enumerate(sorted(far))])
    join(i_b, *i_1)
    tag[0] = "ck"
    c_24 = join(ac(T.L24[:, :], T.LOB[:, :], c_h, 24.0), ac(T.H24[:, :], T.HIB[:, :], c_h, 24.0))

    tag[0] = "lp"
    lp = join(*[ts(T.LP[:, 3 * k:3 * k + 3], T.PO[:, 0:3], 24 * k, A.add, deps=[d_po]) for k in range(2)])
    tag[0] = "lh"
    lsh = join(*[ts(T.LSH[:, 4 * k:4 * k + 4], T.NB[:, 12:16], T.PQ[:, k:k + 1], A.add, deps=c_m + [d_sh]) for k in range(2)])
    tag[0] = "nn"
    nn = tt(T.NN[:, :], T.TR[:, :].indirect(T.LP[:, 0:6]), T.C48[:, :], A.add, deps=lp + d_rel + [i_c])
    tag[0] = "rr"
    rr = cp(T.RR[:, :], T.NN[:, :].indirect(T.LSH[:, :]), deps=[nn] + lsh)
    tag[0] = "as"
    as_ = ac(T.AS[:, :], T.I48[:, :].indirect(T.LP[:, :]), deps=lp + i_48)
    tag[0] = "r0"
    la = [cp(T.LA[:, 0::3], T.RR[:, 0:64:2], deps=[rr]), cp(T.LA[:, 2::3], T.RR[:, 1:64:2], deps=[rr])]
    tag[0] = "qa"
    qa = mms([(T.PT[:, 0:32], T.SH[:, :], T.RR[:, 64:128:2]), (T.PT[:, 0:32], T.SL[:, :], T.RR[:, 65:128:2])], [rr] + c_s)
    tag[0] = "qo"
    qo = join(*(mms([(T.PM[:, 1:72:3], T.SHW[:, :], T.NN[:, 48:96:2]), (T.PM[:, 1:72:3], T.SLW[:, :], T.NN[:, 1:48:2])], [nn] + c_f) +
                mms([(T.PM[:, 0:72:3], T.ID[:, :], T.NN[:, 0:48:2])], [nn, idm]) + mms([(T.PM[:, 2:72:3], T.ID[:, :], T.NN[:, 49:96:2])], [nn, idm])))
    tag[0] = "r1"
    la.append(cp(T.LA[:, 1::3], T.PT[:, 0:32], deps=qa))
    join(*la)
    tag[0] = "bl"
    bl = join(*[ts(T.BL[:, 8 * k:8 * k + 8], T.ON[:, 0::16], T.SQ4[:, k:k + 1], A.mult, 48, A.add, deps=[on, sq4]) for k in range(4)])
    tag[0] = "o1"
    ow = [cp(T.OWN[:, :], T.PM[:, 0:72], deps=qo)]
    tag[0] = "rn"
    c_r = join(ts(T.RN[:, 0:128], T.ON[:, :], T.QF[:, 0:1], A.mult, deps=[on] + c_3),
               ts(T.RN[:, 128:256], T.ON[:, :], T.QF[:, 1:2], A.mult, deps=[on, c_q]))

    for k, p in enumerate(dest):
        a, b = SLW * k, SLW * k + SLW // 2
        tag[0] = "A%d" % k
        x = join(cp(T.SA[:, a:b], T.X[:, :].indirect(T.LA[:, 24 * p:24 * p + 12]), deps=la + [d_x]),
                 ac(T.SA[:, b:a + SLW], T.X[:, :].indirect(T.LA[:, 24 * p + 12:24 * p + 24]), deps=la + [d_x]))
        c, es = OWNW + SLW * (r if r < p else r - 1), feng if p in far else neng
        send([transfer(p, T.SA[:, a:a + SLW], T.W0[:, c:c + SLW], es, "arr0")], len(es), x)
    arr0 = [("sem", "arr0", 2 * len(feng) + len(neng))]
    arr1 = [[("sem", "arr1_%d" % b, len(feng) + len(neng))] for b in range(3)]

    even0, odd0, even1, odd1 = [slice(k, k - k % 2 + 48, 2) for k in (0, 1, 48, 49)]
    bv = CFG["bv"]

    def rows(out, oh, deps):
        return join(*sum([mms([(out[:, 48 * h:48 * h + 48], T.BD[:, 256 * k + 128 * h:256 * k + 128 * h + 128], oh[:, 48 * k:48 * k + 48])
                               for k in range(2)], deps) for h in range(2)], []))

    def parts(uu, one, eight):
        return join(ts(uu[:, 96:192], T.UD[:, 0:96], 8, A.is_ge, eight, A.mult, deps=["ra"]),
                    ts(uu[:, 192:288], T.UD[:, 0:96], 16, A.is_ge, eight, A.mult, deps=["ra"]))

    def natural(P, uu, node, d):
        xs = [uu[:, 96 * k:96 * k + 96] for k in range(3)]
        c0, c1, c2 = [P[:, k:72:3] for k in range(3)]
        return join(*(
            mms([(c0, T.IDB[:, :], node[:, even0])] + [(c0, T.IDB[:, :], x[:, even0]) for x in xs], d) +
            mms([(c1, T.LOB[:, :], node[:, even0]), (c1, T.HIB[:, :], node[:, odd0])] +
                [(c1, T.SHB[:, :], x[:, even1]) for x in xs] + [(c1, T.SLB[:, :], x[:, odd0]) for x in xs], d) +
            mms([(c2, T.IDB[:, :], node[:, odd0])] + [(c2, T.IDB[:, :], x[:, odd1]) for x in xs], d)))

    def halves(out, x):
        return [(out, T.LOB[:, :], x[:, 0::2]), (out, T.HIB[:, :], x[:, 1::2])]

    step = {
        "cw": lambda: join(cp(T.CW[:, 0:24], T.CT[:, 0:24], deps=d_ct),
                           ts(T.CW[:, 24:48], T.CT[:, 24:48], T.HI[:, :], A.mult, deps=d_ct + c_m)),
        "lm": lambda: join(*[ts(T.LM[:, 3 * k:3 * k + 3], T.AC[:, 0:3], 24 * k, A.add, deps=[d_ac]) for k in range(2)]),
        "nb": lambda: [cp(T.NBU[:, :], T.NB[:, :], deps=[d_nb, d_sh])],
        "os": lambda: [tt(T.OS[:, :], T.CW[:, :].indirect(T.LM[:, :]), T.AS[:, :], A.is_equal, deps=["cw", "lm", as_, zc])],
        "ca": lambda: [ac(T.CA[:, :], T.CW[:, :].indirect(T.LP[:, :]), deps=lp + ["cw", zc])],
        "bs": lambda: [ac(T.BD[:, 0:256], T.CW[:, :].indirect(T.BL[:, 0:16]), deps=bl + ["cw", zc])],
        "bw": lambda: [cp(T.BD[:, 256:512], T.CW[:, :].indirect(T.BL[:, 16:32]), deps=bl + ["cw", zc])],
        "ar": lambda: [ac(T.ARM[:, :], T.AT[:, :].indirect(T.NBU[:, :]), deps=i_a + ["nb"])],
        "qs": lambda: join(*sum([mms([(T.PS[:, 48 * h:48 * h + 48], T.RN[:, 128 * k:128 * k + 128], T.OS[:, 48 * k:48 * k + 48])
                                      for k in range(2)], ["os"] + c_r) for h in range(2)], [])),
        "ok": lambda: [tt(T.OK[:, :], T.CA[:, :], T.PS[:, 0:96], A.is_equal, deps=["qs", "ca"])],
        "qk": lambda: rows(T.PK, T.OK, ["ok", "bs", "bw"]),
        "rw": lambda: [cp(T.RW[:, :], T.PK[:, 0:96], deps=["qk"])],
        "qe": lambda: join(*sum([mms(halves(T.PJ[:, 8 * k:8 * k + 8], T.ARM[:, 192 + 16 * p:208 + 16 * p]), ["ar"] + c_h)
                                 for k, p in enumerate(far)], [])),
        "le": lambda: [ts(T.LE[:, :], T.PJ[:, 0:16], 8, A.mult, T.QR[:, :], A.add, deps=["qe"] + c_3)],
        "nu": lambda: [cp(T.NSU[:, 0:1], T.NS[:, 0:1], deps=[("sem", "arrs", len(aeng))])],
        "nt": lambda: [ts(T.AT1[:, 48 + 16 * near[0]:64 + 16 * near[0]], T.AT[:, 0:48].indirect(T.NSU[:, 0:1]), 48, A.add, 8, A.mult,
                          deps=i_a + ["nu"])],
        "an": lambda: [ac(T.AR1[:, :], T.AT1[:, :].indirect(T.NBU[:, 0:12]), deps=i_1 + ["nb", "nt"])],
        "qj": lambda: mms(halves(T.PJ[:, 0:96], T.AR1[:, :]), ["an", "le"] + c_h),
        "lf": lambda: [ts(T.LF[:, :], T.PJ[:, 0:96], T.QR[:, :], A.add, deps=["qj"] + c_3)],
        "xs": lambda: [ac(T.W0[:, 24 * bv:OWNW], T.X[:, :].indirect(T.OWN[:, bv * 3 // 2:72]), deps=ow + [d_x])],
        "xv": lambda: [cp(T.W0[:, 0:24 * bv], T.X[:, :].indirect(T.OWN[:, 0:bv * 3 // 2]), deps=ow + [d_x])] if bv else [],
        "ms": lambda: [ac(T.MS[:, :], T.I48[:, :].indirect(T.LM[:, :]), deps=["lm"] + i_48)],
        "oa": lambda: [tt(T.OA[:, :], T.TR[:, :].indirect(T.LP[:, :]), T.MS[:, :], A.is_equal, deps=["ms"])],
        "qy": lambda: rows(T.PT, T.OA, ["oa", "bs", "bw"] + la),
        "ra": lambda: join(ac(T.UD[:, 0:96], T.PT[:, 0:96], ["qy"]), ac(T.UU[:, 0:96], T.PT[:, 0:96], ["qy"], 3.0)),
        "uu": lambda: parts(T.UU, 3, -23),
        "qz": lambda: natural(T.PM, T.UU, T.CB, ["uu", i_b] + ow + c_h),
        "ly": lambda: [cp(T.LY[:, :], T.PM[:, 0:72], deps=["qz"])],
        "ud": lambda: parts(T.UD, 1, BLK - 8),
        "qd": lambda: natural(T.PK, T.UD, T.AR1[:, 144:192], ["ud", "an", "rw"] + c_h),
        "ld": lambda: [cp(T.LD[:, :], T.PK[:, 0:72], deps=["qd"])],
    }
    picks = [((T.LOB, even0), (T.SLB, odd0)), ((T.LOB, even1), (T.HIB, odd0)), ((T.SHB, even1), (T.HIB, odd1))]
    for b in range(3):
        step["j%d" % b] = lambda b=b: mms([(T["PL%d" % b][:, 0:96], m[:, :], T.ARM[:, h:192:2]) for h, m in enumerate((T.L24, T.H24))],
                                          ["ar"] + c_24, last=False)
        step["q%d" % b] = lambda b=b: mms([(T["PL%d" % b][:, 24 * n:24 * n + 24], m[:, :], T.RW[:, c]) for n in range(4) for m, c in picks[b]],
                                          ["rw"] + c_h, first=False)
        step["l%d" % b] = lambda b=b: [cp(T.LC[:, 96 * b:96 * b + 96], T["PL%d" % b][:, 0:96], deps=["q%d" % b])]

    banks = [[T.PS, ["ok"]], [T.PL0, ["l0"]], [T.PL1, ["l1"]], [T.PL2, ["l2"]], [T.PJ, ["lf"]], [T.PK, ["ld" if CFG["four"] < 48 else "rw"]]]
    turn = [0]
    own0 = ["xs", "xv"]
    P = {}
    at = 0
    for k, (rd, b, i0, n, kv) in CFG["P"].items():
        j = {"rd": rd, "b": b, "i0": i0, "n": n, "kv": kv, "w": 8 * n, "at": at, "last": 2 if rd == 0 or i0 < CFG["four"] else 1}
        if rd == 0:
            win, lst, c0 = T.W0[:, :], T.LC, 96 * b + i0 // 2
            j["deps"], j["out"] = ["l%d" % b] + own0 + arr0, T.W1[:, BLK * b + 8 * i0:BLK * b + 8 * (i0 + n)]
        else:
            win, lst, c0 = T.W1[:, BLK * b:BLK * b + BLK], T.LF, i0 // 2
            j["deps"], j["out"] = ["lf", "W%d" % b] + arr1[b], T.MP[:, 24 * i0 + b:24 * (i0 + n):3]
        j["src"] = [win.indirect(lst[:, c0 + 24 * m:c0 + 24 * m + n // 2]) for m in range(4)]
        j["G"] = [T["G%d" % m][:, at:at + 8 * n] for m in range(3)]
        j["H"] = [T["H%d" % m][:, at:at + 8 * n] for m in range(2)]
        at += 8 * n
        P[k] = j

    def scalar_step(k, m):
        j = P[k]
        named[k + ("g0" if m == 0 else "s%d" % m)] = [ac(j["G"][m], j["src"][j["last"] + 1 - m], j["deps"])]

    def tensor_step(k, m):
        j = P[k]
        bank = banks[turn[0] % len(banks)]
        turn[0] += 1
        j["P%d" % m] = bank[0][:, 0:j["w"]]
        named[k + "g%d" % m] = mms([(j["P%d" % m], T.ID[:, :], j["G"][m])], [k + "s%d" % m, idm] + bank[1])
        bank[1] = [k + "v%d" % (j["kv"] + m - 1)]

    def vector_step(k, m):
        j = P[k]
        kv = j["kv"]
        out = j["out"] if m == j["last"] else j["H"][m]
        prev = (j["G"][0], k + "g0") if m == 0 else (j["H"][m - 1], k + "v%d" % (m - 1))
        if m < kv:
            x = tt(out, j["src"][m], prev[0], A.max, j["deps"] + [prev[1]])
        else:
            u = m - kv + 1
            x = tt(out, prev[0], j["P%d" % u], A.max, [prev[1], k + "g%d" % u])
        named[k + "v%d" % m] = [x]
        if m == j["last"]:
            named.setdefault("WM"[j["rd"]] + str(j["b"]), []).append(x)
            named[k + "done"] = [x]

    def shown(b, q, lo, hi):
        named.setdefault("E%d" % b, []).append((ac if q == "s" else cp)(
            T.EX[:, 256 * b + 8 * lo:256 * b + 8 * hi], T.W1[:, BLK * b:BLK * b + 384].indirect(T.LE[:, lo // 2:hi // 2]), ["le", "W%d" % b]))

    def shown_parts(b, q):
        ks = [k for k in P if P[k]["rd"] == 0 and P[k]["b"] == b]
        c = P[ks[0]]["at"]
        if q == "s":
            named["EG%d" % b] = [ac(T.EG[:, 256 * b:256 * b + 256], T.G1[:, c:c + 384].indirect(T.LE[:, :]), ["le"] + [k + "s1" for k in ks])]
        else:
            named["E%d" % b] = [tt(T.EX[:, 256 * b:256 * b + 256], T.H1[:, c:c + 384].indirect(T.LE[:, :]), T.EG[:, 256 * b:256 * b + 256],
                                   A.max, ["le", "EG%d" % b] + [k + "v1" for k in ks])]

    finals, fourth = [], []

    def framed(b):
        return ["ly"] + [x + "done" for x in P if P[x]["rd"] == 1 and P[x]["i0"] < b]

    def final(q, a, b):
        finals.append((a, b, (ac if q == "s" else cp)(T.YB[:, 24 * a:24 * b], T.MP[:, 0:24 * b].indirect(T.LY[:, a * 3 // 2:b * 3 // 2]), framed(b))))

    def direct(a, b):
        fourth.append((a, b, ac(T.DB[:, 24 * a:24 * b], T.W1[:, :].indirect(T.LD[:, a * 3 // 2:b * 3 // 2]),
                                ["ld", "W0", "W1", "W2"] + sum(arr1, []))))

    def joined(a, b):
        finals.append((a, b, tt(T.YB[:, 24 * a:24 * b], T.MP[:, 0:24 * b].indirect(T.LY[:, a * 3 // 2:b * 3 // 2]), T.DB[:, 24 * a:24 * b],
                                A.max, framed(b) + [d for lo, hi, d in fourth if lo < b and a < hi])))

    early = set(o["tag"] for o in ops)
    for q in "tsv":
        for w in CFG[q.upper()].split():
            tag[0] = w
            w, lo, hi = (w.split(":") + [0, 32])[:3]
            if w in early:
                continue
            if w[0] == "E":
                shown(int(w[1]), q, int(lo), int(hi))
            elif w[0] == "F":
                shown_parts(int(w[1]), q)
            elif w[0] == "Y":
                final(q, int(lo), int(hi))
            elif w[0] in "DZ":
                (direct if w[0] == "D" else joined)(int(lo), int(hi))
            elif w in step:
                named[w] = step[w]()
            else:
                {"t": tensor_step, "s": scalar_step, "v": vector_step}[q](w[0], int(w[1]))

    for a, b in (("bs", "bw"), ("xs", "xv")):
        join(*(named[a] + named[b]))
    join(*(lp + lsh))
    join(idm, *c_f)
    half = len(feng) // 2
    for w in CFG["G"].split():
        b = int(w[1])
        c, arr = BLK * b, "arr1_%d" % b
        if w[0] == "n":
            send([transfer(near[0], T.W1[:, c:c + 384], T.W1[:, c + 384:c + 768], neng, arr)], len(neng), ["W%d" % b])
        else:
            c += 768 + 128 * sorted([r] + near).index(r)
            send([transfer(p, T.EX[:, 256 * b + 128 * k:256 * b + 128 * k + 128], T.W1[:, c:c + 128], feng[half * k:half * k + half], arr)
                  for k, p in enumerate(far)], len(feng), ["E%d" % b])
    stores = []
    for a, b in zip(CFG["stores"], CFG["stores"][1:]):
        stores.append(ld("y", T.y[:, 24 * a:24 * b], T.YB[:, 24 * a:24 * b], [x for lo, hi, x in finals if lo < b and a < hi]))
    op("y", None, stores, "w")
    op("g", None, [("sem", "left", left[0])], "w")

    for o in ops:
        o["deps"] = sum([named[d] if isinstance(d, str) else [d] for d in o["deps"]], [])
    if "hook" in CFG:
        CFG["hook"](ops)
    used, total = set(), {}
    for o in ops:
        used.update(ops[d]["grp"] for d in o["deps"] if not isinstance(d, tuple))
    for o in ops:
        total[o["grp"]] = total.get(o["grp"], 0) + (16 if o["kind"] == "d" else 1)
    order = {q: CFG.get(q.upper(), "").split() for q in queues}
    seq = sorted(ops, key=lambda o: order[o["q"]].index(o["tag"]) if o["q"] in "vst" and o["kind"] == "c" else -1)
    names = {k: "x%d" % n for n, k in enumerate(sorted(used))}
    done = {q: {} for q in queues}

    def wait(q, name, val):
        if done[q].get(name, 0) < val:
            queues[q].wait_ge(T.sem[name], val)
            done[q][name] = val

    for o in seq:
        for d in o["deps"]:
            if isinstance(d, tuple):
                wait(o["q"], d[1], d[2])
            else:
                k = ops[d]["grp"]
                wait(o["q"], names[k], total[k])
        if o["kind"] != "w":
            ins = o["f"]()
            if o["grp"] in names:
                ins.then_inc(T.sem[names[o["grp"]]], 16 if o["kind"] == "d" else 1)
